import numpy as np, ml_dtypes
CORES = [16,18,20,22]
N = 4
BF = ml_dtypes.bfloat16
W, P, RO, L = 3072, 1, 6, 256
Q = 1.0
def parts(rng):
    share = rng.choice(np.array([0.015, 0.025, 0.04]), (N, 8, 1, 1)) * Q
    r = np.where(rng.random((N, 8, 16, W)) < share, rng.integers(5, 16, (N, 8, 16, W)), rng.integers(0, 5, (N, 8, 16, W)))
    hot = (rng.random((N, 8, 1, W)) < 0.004 * Q) & (rng.random((N, 8, 16, W)) < 0.7)
    r = np.where(hot, 15, r)
    return r, rng.integers(0, 256, (N, 8, 16, W)), rng.integers(0, W, (N, 8, 16, W)), rng.integers(0, W, (N, 8, 16, L))
def pack(r, x, k, s):
    return {"rec": np.ascontiguousarray(r.reshape(N, 128, W)).astype(np.float32).astype(BF), "wealth": np.ascontiguousarray(x.reshape(N, 128, W)).astype(np.float32).astype(BF),
            "kin": np.ascontiguousarray(k.reshape(N, 128, W)).astype(np.int32), "slips": np.ascontiguousarray(s.reshape(N, 128, L)).astype(np.int32)}
def setup_inputs(rng):
    r, x, k, s = parts(rng)
    return pack(r, x, k, s)
def setup_inputs_spread(rng):
    e = np.exp2(4.3 + 3.9 * rng.random((N, 8, 16, 1))) / Q
    r = np.minimum((16 * rng.random((N, 8, 16, W)) ** e).astype(np.int64), 15)
    x = np.minimum((np.exp2(8 * rng.random((N, 8, 1, W))) * rng.random((N, 8, 16, W))).astype(np.int64), 255)
    k = np.minimum((W * rng.random((N, 8, 16, W)) ** 2).astype(np.int64), W - 1)
    s = np.minimum((W * rng.random((N, 8, 16, L)) ** (1 + rng.random((N, 8, 1, L)))).astype(np.int64), W - 1)
    return pack(r, x, k, s)
def setup_inputs_ends(rng):
    r = 15 * (rng.random((N, 8, 16, W)) < 0.02 * Q)
    r = np.where(rng.random((N, 8, 1, W)) < 0.004 * Q, 15, r)
    w = rng.random((N, 8, 1, W)); x = 255 * np.where(w < 0.4, 0, np.where(w < 0.7, 1, rng.integers(0, 2, (N, 8, 16, W))))
    u = rng.random((N, 8, 16, W))
    k = np.where(u < 0.36, 0, np.where(u < 0.72, W - 1, np.where(u < 0.78, W - 2, rng.integers(0, W, (N, 8, 16, W)))))
    for first, places in ((1, ((2, W - 2), (15, W - 1))), (3, ((4, W - 1), (9, 5), (12, 5))), (6, ((4, 5), (9, W - 1)))):
        c = np.zeros((16, 1), np.int64)
        for m, v in places: c[m, 0] = v
        k[:, :, :, first::8] = c; x[:, :, :, first::8] = 0
    m = (np.arange(W) & 4) == 4
    k[:, 7] = np.where(m & (k[:, 7] == W - 1), 0, k[:, 7])
    a, b = W - 600, W - 344
    k[:, :, :, a:b] = 0; r[:, :, :, a:b] = 0; x[:, :, :, a:b] = 0
    k[:, :, :, W - 40:W - 24] = 0; r[:, :, :, W - 40:W - 24] = 0; x[:, :, :, W - 40:W - 24] = 0; k[:, :, 15, W - 32:W - 24] = W - 1
    r[:, :, :, 0] = 0; r[:, :, :, W - 1] = 15 * (rng.random((N, 8, 16)) < rng.choice(np.array([0.05, 0.15, 0.3]), (N, 8, 1))); r[:, 7, :, W - 1] = 15
    r[:, :, :, W - 2] = 0; r[:, :, :, 5] = 0
    x[:, :, :, 0] = 0; x[:, :, :, W - 1] = 255; x[:, :, :, 5] = 255; x[:, :, :, W - 2] = 255; x[:, :, 15, W - 2] = 254
    u = rng.random((N, 8, 16, L)); s = np.where(u < 0.35, 0, np.where(u < 0.7, W - 1, rng.integers(1, W - 600, (N, 8, 16, L))))
    s[:, :, :, 112:128] = W - 1
    for q in range(2):
        for g in range(8): s[q, g, :, 240:] = a + rng.permutation(256).reshape(16, 16)
    p = np.arange(16); s[N - 1, 7, :, 255] = np.where((p & 1) == 0, W - 40 + (p >> 1), W - 32 + (p >> 1))
    return pack(r, x, k, s)
def setup_inputs_corners(rng):
    r, x, k, s = parts(rng); own = np.arange(W); lane = np.arange(L)
    k[:, :4] = own
    n = rng.choice(np.array([0, 1, 3, 7, 8, 9, 11, 12, 13, 16]), (1, 4, 1, W)); order = np.argsort(rng.random((1, 4, 16, W)), axis=2)
    high = np.where(rng.random((N, 4, 16, W)) < 0.7, 15, rng.integers(6, 16, (N, 4, 16, W)))
    low = np.where(rng.random((N, 4, 16, W)) < 0.15, 5, rng.integers(0, 5, (N, 4, 16, W)))
    high[:, 1] = 6; low[:, 1] = 5; high[:, 2] = 6 + (own & 7); low[:, 2] = 5 + (own & 7)
    r[:, :4] = np.where(order < n, high, low)
    s[:, :2] = lane + 256 * rng.integers(0, W // 256, (N, 2, 16, L))
    s[:, 4] = np.repeat(rng.integers(0, W, (N, 1, 16)), 16, axis=2)
    for q in range(N):
        if (q & 1) == 0: s[q, 5] = rng.integers(0, W)
        else: s[q, 5] = lane + 256 * rng.integers(0, W // 256, (16, L))
    k[:, 6] = rng.choice(np.array([0, W - 1, W // 2]), (N, 1, W))
    z = rng.integers(0, 3, (N, 16, W)); k[:, 7] = np.where(z == 0, 0, np.where(z == 1, W - 1, own))
    r[:, 6:, :, [0, W - 1, W // 2]] = np.where(rng.random((N, 2, 16, 3)) < 0.2, 15, rng.integers(0, 5, (N, 2, 16, 3)))
    s[:, 7] = np.where(rng.random((N, 16, L)) < 0.1, rng.choice(np.array([0, W - 1]), (N, 16, L)), s[:, 7])
    x[:, 1] = 255; x[:, 2] = 255 * rng.integers(0, 2, (N, 1, W))
    return pack(r, x, k, s)
def setup_inputs_alike(rng):
    r, x, k, s = parts(rng)
    pool = np.repeat(rng.integers(0, W, (N, 8, 16, 6)), 16, axis=2)
    few = np.take_along_axis(pool, rng.integers(0, 6, (N, 8, L, 16)), 3).transpose(0, 1, 3, 2)
    s[:, ::2] = few[:, ::2]
    s[:, 1::4, :, 1::2] = np.roll(s[:, 1::4, :, 0::2], 5, axis=2)
    s[:, 3] = W - 1 - rng.integers(0, 40, (N, 16, L))
    k[:, 1::2, 8:] = k[:, 1::2, :8]
    x = np.take_along_axis(rng.choice(np.array([0, 128, 255]), (N, 8, 16, 5)), rng.integers(0, 5, (N, 8, 1, W)), 3)
    return pack(r, x, k, s)
def setup_inputs_full(rng):
    r, x, k, s = parts(rng); own = np.arange(W); lane = np.arange(L); bag = (own >> 4) & 15
    z = 2 * rng.integers(0, 8, N) + 1
    r[:, :3] = rng.integers(0, 5, (N, 3, 16, W))
    even = own[(own & 16) == 0]; r[:, 1, bag[even], even] = 15; k[:, 1] = k[:, 1] | 16
    hot = np.repeat((bag[None, :] == z[:, None])[:, None, :], 8, axis=1)
    hot[:, :2, :256] = False; hot[:, 2, :256:2] = False
    r = np.where(hot[:, :, None, :], 15, r)
    named = np.take_along_axis(hot, k.reshape(N, 8, 16 * W), 2).reshape(N, 8, 16, W); k = np.where(named, k ^ 32, k)
    s[:, :3] = lane + 256 * rng.integers(0, W // 256, (N, 3, 16, L))
    inbag = (lane >> 4)[None, :] == z[:, None]
    first = np.arange(16)[:, None] == ((5 * (lane & 15)) & 15)[None, :]
    s = np.where(inbag[:, None, None, :], lane + 256 * np.where(first, 0, rng.integers(1, W // 256, (N, 8, 16, L))), s)
    return pack(r, x, k, s)
def check_inputs(d):
    bad = []
    for k, lo, hi in (("rec", 0, 15), ("wealth", 0, 255), ("kin", 0, W - 1), ("slips", 0, W - 1)):
        v = np.asarray(d[k]).astype(np.float64)
        if not (np.min(v) >= lo and np.max(v) <= hi): bad.append("range of " + k)
        elif np.any(v != np.floor(v)): bad.append("whole numbers of " + k)
    return bad
def reference(rec, wealth, kin, slips):
    R = rec.astype(np.float32).astype(np.int64).reshape(N, 8, 16, W); X = wealth.astype(np.float32).astype(np.int64).reshape(N, 8, 16, W)
    K = kin.astype(np.int64).reshape(N, 8, 16, W); S = slips.astype(np.int64).reshape(N, 8, 16, L)
    lane = np.arange(L); b = lane >> 4; j = lane & 15; a = np.zeros((N, 16), np.int64)
    lower = lane[None, :] < lane[:, None]
    def picks(tab, ks):
        return np.take_along_axis(tab, ks.reshape(8, 1, 16 * L), 2).reshape(8, 16, 16, L)
    for t in range(RO):
        T = 8 + t; later = []
        for r in range(N):
            o = (a[r][b] + 5 * j + t) & 15
            c = S[r][:, o, lane]
            ci = c[:, None, :]
            counts = ~np.any((c[:, :, None] == c[:, None, :]) & lower[None], axis=2)
            kc = np.take_along_axis(K[r], ci, 2)
            M = np.maximum(np.take_along_axis(R[r], ci, 2), np.max(picks(R[r], kc), axis=2))
            for u in range(P):
                q = (r + 1 + (P * t + u) % (N - 1)) % N
                M = np.maximum(M, np.max(picks(R[q], np.take_along_axis(K[q], ci, 2)), axis=2))
            f = np.sum(M >= T - 2, axis=1)
            bar = (M[:, b, lane] >= T - 3) | (f >= 8)
            barred = counts & bar; inst = counts & ~bar
            torn = inst | (barred & (f >= 12))
            nxt = np.zeros((8, L), bool); nxt[:, :L - 16] = torn[:, 16:]
            moved = barred & (f < 12) & ((f & 1) == 1) & nxt
            sc = np.sum(np.maximum(picks(X[r], kc) - np.take_along_axis(X[r], ci, 2)[:, :, None, :], 0), axis=1)
            best = np.take_along_axis(kc, np.argmax(sc, axis=1)[:, None, :], 1)[:, 0]
            new = np.where(torn | moved, best, c)
            new[:, 16:] = np.where(moved[:, :L - 16], c[:, :L - 16], new[:, 16:])
            later.append((o, c, inst, new))
        for r in range(N):
            o, c, inst, new = later[r]
            S[r][:, o, lane] = new
            gi, li = np.nonzero(inst)
            R[r][gi, b[li], c[gi, li]] = T
            K[r][gi, t, c[gi, li]] = c[gi, li ^ 1]
            a[r] = np.sum(inst.reshape(8, 16, 16), axis=(0, 2))
    return {"yr": R.reshape(N, 128, W).astype(np.float32).astype(BF), "ys": S.reshape(N, 128, L).astype(np.float32)}

@@ -1,0 +1,410 @@
+import math
+from concourse.mybir import AluOpType as A
+from concourse.mybir import ActivationFunctionType as F
+from concourse.mybir import AxisListType
+
+RO = 6
+W = 3072
+WD = W + 256
+BASE = 1.75
+XB = [256 * b - 8 * b * (b - 1) for b in range(17)]
+
+SCRATCH = {
+    "recs": ("sbuf", [128, W], "bfloat16"), "kinI": ("sbuf", [128, W], "int32"), "slI": ("sbuf", [128, 256], "int32"),
+    "E": ("sbuf", [128, WD], "bfloat16"), "K": ("sbuf", [128, WD], "float32"), "Wt": ("sbuf", [128, W], "bfloat16"),
+    "IOTA": ("sbuf", [128, W], "float32"), "LN": ("sbuf", [128, W], "float32"),
+    "YR": ("sbuf", [128, W], "bfloat16"), "YR2": ("sbuf", [128, W], "bfloat16"),
+    "GE": ("sbuf", [128, 4096], "bfloat16"), "FE": ("sbuf", [128, 4096], "bfloat16"), "X": ("sbuf", [128, 4096], "bfloat16"), "S1s": ("sbuf", [128, 256], "float32"), "LM": ("sbuf", [128, 16], "uint16"),
+    "Z": ("sbuf", [128, 512], "float32"), "ZT": ("sbuf", [128, 512], "float32"), "ysb": ("sbuf", [128, 256], "float32"),
+    "kc2": ("sbuf", [128, 512], "float32"), "kTr": ("sbuf", [128, 512], "float32"),
+    "kcu": ("sbuf", [128, 256], "uint16"), "fku": ("sbuf", [128, 256], "uint16"), "kTu": ("sbuf", [128, 256], "uint16"),
+    "kTi": ("sbuf", [128, 256], "int32"), "hi": ("sbuf", [128, 256], "int32"), "lo": ("sbuf", [128, 256], "int32"),
+    "kHL": ("sbuf", [128, 512], "float32"), "sHL": ("sbuf", [128, 512], "float32"),
+    "bI": ("sbuf", [128, 32], "int32"), "bI2": ("sbuf", [128, 32], "int32"), "b64": ("sbuf", [128, 16], "float32"),
+    "best": ("sbuf", [128, 16], "float32"), "db": ("sbuf", [128, 16], "float32"), "dp": ("sbuf", [128, 16], "float32"),
+    "cT2": ("sbuf", [128, 32], "uint16"), "cTf": ("sbuf", [128, 16], "float32"), "cTg": ("sbuf", [128, 16], "float32"),
+    "cbu": ("sbuf", [128, 256], "uint16"), "cbf": ("sbuf", [128, 256], "float32"), "kcf": ("sbuf", [128, 256], "float32"),
+    "kd": ("sbuf", [128, 256], "float32"), "kd2": ("sbuf", [128, 256], "float32"), "iR": ("sbuf", [128, 256], "float32"),
+    "Ec": ("sbuf", [128, 256], "bfloat16"), "wc": ("sbuf", [128, 256], "bfloat16"),
+    "EQT": ("sbuf", [128, XB[16]], "bfloat16"), "dupb": ("sbuf", [128, 256], "bfloat16"),
+    "MJc": ("sbuf", [128, 256], "float32"), "cs": ("sbuf", [128, 256], "float32"),
+    "sl1": ("sbuf", [128, 16], "float32"), "sl2": ("sbuf", [128, 16], "float32"), "SL": ("sbuf", [128, 16], "uint16"),
+    "X1": ("sbuf", [128, 256], "bfloat16"), "X2": ("sbuf", [128, 256], "bfloat16"),
+    "iD": ("sbuf", [128, 256], "bfloat16"), "iT": ("sbuf", [128, 256], "bfloat16"), "cn": ("sbuf", [128, 1], "float32"),
+    "qm": ("sbuf", [128, 256], "float32"), "zs": ("sbuf", [128, 256], "float32"),
+    "z4": ("sbuf", [128, 16], "int32"), "zy": ("sbuf", [128, 16], "int32"), "od": ("sbuf", [128, 16], "int32"),
+    "a1": ("sbuf", [128, 16], "float32"), "b3": ("sbuf", [128, 16], "float32"), "tn": ("sbuf", [128, 16], "float32"),
+    "mv0": ("sbuf", [128, 16], "float32"), "mv": ("sbuf", [128, 16], "float32"), "tm": ("sbuf", [128, 16], "float32"),
+    "u1": ("sbuf", [128, 16], "float32"), "v1": ("sbuf", [128, 16], "float32"), "nT": ("sbuf", [128, 16], "float32"),
+    "uk": ("sbuf", [128, 1], "int32"), "offs": ("sbuf", [128, 2], "uint16"),
+    "pI": ("sbuf", [128, 1], "int32"), "pF": ("sbuf", [128, 1], "float32"), "xI": ("sbuf", [128, 1], "int32"), "xF": ("sbuf", [128, 1], "float32"),
+    "gI": ("sbuf", [128, 1], "int32"), "gF": ("sbuf", [128, 1], "float32"), "hI": ("sbuf", [128, 1], "int32"), "hF": ("sbuf", [128, 1], "float32"),
+    "colA": ("sbuf", [128, 1], "float32"), "colB": ("sbuf", [128, 1], "float32"), "colC": ("sbuf", [128, 1], "float32"), "colD": ("sbuf", [128, 1], "float32"),
+    "rI": ("sbuf", [128, 256], "int32"), "rJ": ("sbuf", [128, 256], "int32"), "rB": ("sbuf", [128, 256], "int32"), "rH": ("sbuf", [128, 32], "int32"),
+    "MJ": ("sbuf", [128, 256], "float32"), "DB": ("sbuf", [128, 256], "float32"), "NB": ("sbuf", [128, 256], "float32"), "tq": ("sbuf", [128, 256], "float32"),
+    "BO": ("sbuf", [128, 128], "bfloat16"), "BOh": ("sbuf", [128, 128], "bfloat16"), "BO32": ("sbuf", [128, 128], "bfloat16"),
+    "ID": ("sbuf", [128, 128], "bfloat16"), "ID64": ("sbuf", [128, 128], "bfloat16"), "IDf": ("sbuf", [128, 128], "float32"), "SelC": ("sbuf", [128, 128], "float32"),
+    "QJ": ("sbuf", [128, 144], "bfloat16"), "TIE": ("sbuf", [128, 256], "bfloat16"),
+    "lane": ("sbuf", [128, 16], "float32"), "dm": ("sbuf", [128, 16], "float32"), "wcol": ("sbuf", [128, 16], "float32"),
+    "riF": ("sbuf", [128, 256], "float32"), "THR": ("sbuf", [128, 256], "float32"), "THJ": ("sbuf", [128, 256], "float32"),
+    "DT": ("sbuf", [128, RO * 256], "bfloat16"), "Dlt": ("sbuf", [128, 256], "float32"), "Rt": ("sbuf", [128, 8], "float32"), "CU": ("sbuf", [128, 8], "float32"),
+    "eb": ("sbuf", [128, 4], "float32"),
+    "D0": ("sbuf", [128, 512], "float32"), "L1": ("sbuf", [128, 32], "uint16"), "L2": ("sbuf", [128, 32], "uint16"), "LZ": ("sbuf", [128, 32], "uint16"), "LQ": ("sbuf", [128, 16], "uint16"),
+    "cTu": ("sbuf", [128, 16 * RO], "uint16"), "ql": ("sbuf", [128, 16 * RO], "uint16"),
+    "fs": ("sbuf", [128, 256 * RO], "bfloat16"), "rl": ("sbuf", [128, 256 * RO], "bfloat16"),
+    "pES": ("psum", [128, 512], "float32"), "pFS": ("psum", [128, 512], "float32"), "pEQ": ("psum", [128, 512], "float32"),
+    "pS1": ("psum", [128, 512], "float32"), "pZ": ("psum", [128, 512], "float32"), "pU": ("psum", [128, 512], "float32"),
+}
+SEMAPHORES = ["sv", "ss", "sp", "sg", "ls", "dsl", "dsh", "dun", "dys", "dw"] + ["dk%d" % i for i in range(4)] + ["dr%d" % i for i in range(2)] + ["dy%d" % i for i in range(4)] \
+    + ["qa%d" % t for t in range(RO)] + ["ra%d" % t for t in range(RO)]
+
+
+def rank_program(g, core, T, topo):
+    rank = T.rank_of(core)
+    if rank is None:
+        return
+    sem = T.sem
+    ENG = {"V": g.vector, "S": g.scalar, "P": g.tensor, "G": g, "Y": g.sync}
+    SEM = {"V": "sv", "S": "ss", "P": "sp", "G": "sg"}
+    cnt = {}
+    clock = {"V": {}, "S": {}, "P": {}, "G": {}, "Y": {}}
+    snap = {}
+    lastw = {}
+    lastr = {}
+
+    def dep(q, r, w):
+        need = {}
+
+        def add(tok, war):
+            s, n = tok
+            if war and q == "P" and s == "sp":
+                return
+            if need.get(s, 0) < n:
+                need[s] = n
+        for k in r:
+            if k in lastw:
+                add(lastw[k], False)
+        for k in w:
+            if k in lastw:
+                add(lastw[k], True)
+            for s, n in lastr.get(k, {}).items():
+                add((s, n), True)
+        ck = clock[q]
+        for s in sorted(need, key=lambda s: -len(snap.get((s, need[s]), {}))):
+            n = need[s]
+            if ck.get(s, 0) < n:
+                ENG[q].wait_ge(sem[s], n)
+                ck[s] = n
+                for s2, n2 in snap.get((s, n), {}).items():
+                    if ck.get(s2, 0) < n2:
+                        ck[s2] = n2
+
+    def mark(q, tok, r, w):
+        snap[tok] = dict(clock[q])
+        for k in w:
+            lastw[k] = tok
+            lastr[k] = {}
+        for k in r:
+            d = lastr.setdefault(k, {})
+            if d.get(tok[0], 0) < tok[1]:
+                d[tok[0]] = tok[1]
+
+    def op(q, fn, w, r):
+        w, r = w.split(), r.split()
+        dep(q, r, w)
+        s = SEM[q]
+        fn().then_inc(sem[s], 1)
+        cnt[s] = cnt.get(s, 0) + 1
+        mark(q, (s, cnt[s]), r, w)
+
+    def dmas(q, pairs, s, w, r):
+        w, r = w.split(), r.split()
+        dep(q, r, w)
+        for o, i in pairs:
+            ENG[q].dma_start(o, i).then_inc(sem[s], 16)
+            cnt[s] = cnt.get(s, 0) + 16
+        mark(q, (s, cnt[s]), r, w)
+
+    def ts(w, r, out, in0, s1, s2, op0, op1=None):
+        if op1 is None:
+            op("V", lambda: g.vector.tensor_scalar(out, in0, s1, None, op0), w, r)
+        else:
+            op("V", lambda: g.vector.tensor_scalar(out, in0, s1, s2, op0, op1), w, r)
+
+    def tt(w, r, out, a, b, o):
+        op("V", lambda: g.vector.tensor_tensor(out, a, b, o), w, r)
+
+    def cp(w, r, out, in_):
+        op("V", lambda: g.vector.tensor_copy(out, in_), w, r)
+
+    def fill(w, ap, v):
+        op("V", lambda: g.vector.memset(ap, v), w, "")
+
+    def scan(w, r, out, d1):
+        n = 256
+        op("V", lambda: g.vector.tensor_tensor_scan(out, T.D0[:, 0:n], d1, 0.0, A.mult, A.add), w, r + " D0")
+
+    def scanmax(w, r, out, d1):
+        op("V", lambda: g.vector.tensor_tensor_scan(out, T.D0[:], d1, 0.0, A.mult, A.max), w, r + " D0")
+
+    def vtr(w, r, out, in_):
+        op("V", lambda: g.vector.transpose(out, in_), w, r)
+
+    def act(w, r, out, in_, f, bias=0.0, scale=1.0):
+        op("S", lambda: g.scalar.activation(out, in_, f, bias=bias, scale=scale), w, r)
+
+    def mm(w, r, out, l, x, st, sp):
+        op("P", lambda: g.tensor.matmul(out, l, x, st, sp), w, r)
+
+    dmas("Y", [(T.slI[:], T.slips[:])], "dsl", "slI", "")
+    for i in range(4):
+        a, b = 768 * i, 768 * (i + 1)
+        dmas("Y" if i < 2 else "S", [(T.kinI[:, a:b], T.kin[:, a:b])], "dk%d" % i, "kinI%d" % i, "")
+    for i in range(2):
+        a, b = 1536 * i, 1536 * (i + 1)
+        dmas("Y", [(T.recs[:, a:b], T.rec[:, a:b])], "dr%d" % i, "recs%d" % i, "")
+    dmas("S", [(T.Wt[:], T.wealth[:])], "dw", "Wt", "")
+
+    op("G", lambda: g.iota(T.pI[:], [[0, 1]], 0, 1), "pI", "")
+    op("G", lambda: g.iota(T.rI[:], [[1, 256]], 0, 0), "rI", "")
+    op("G", lambda: g.iota(T.IOTA[:], [[1, W]], 0, 0, allow_small_or_imprecise_dtypes=True), "IOTA", "")
+    SH, AND = A.arith_shift_right, A.bitwise_and
+    ts("xI", "pI", T.xI[:], T.pI[:], 15, None, AND)
+    ts("hI", "pI", T.hI[:], T.pI[:], 16, None, AND)
+    ts("rH", "rI", T.rH[:], T.rI[:, 0:32], 1, None, SH)
+    ts("rJ", "rI", T.rJ[:], T.rI[:], 15, None, AND)
+    cp("xF", "xI", T.xF[:], T.xI[:])
+    cp("hF", "hI", T.hF[:], T.hI[:])
+    ts("colC", "xF", T.colC[:], T.xF[:], 16.0, None, A.mult)
+    ts("colA", "xF hF", T.colA[:], T.xF[:], 32.0, T.hF[:], A.mult, A.add)
+    tt("colB", "xF hF", T.colB[:], T.xF[:], T.hF[:], A.add)
+    ts("L1", "rH xF", T.L1[:], T.rH[:], 16.0, T.xF[:], A.mult, A.add)
+    ts("LZ", "rJ colA", T.LZ[:], T.rJ[:, 0:32], T.colA[:], None, A.add)
+    ts("LQ", "rI colB", T.LQ[:], T.rI[:, 0:16], 32.0, T.colB[:], A.mult, A.add)
+    ts("L2", "rH colC", T.L2[:], T.rH[:], T.colC[:], None, A.add)
+    cp("offs", "xF", T.offs[:, 0:1], T.xF[:])
+    cp("kc2", "slI L1", T.kc2[:], T.slI[:].indirect(T.L1[:, 0:32]))
+    vtr("kTr", "kc2", T.kTr[:], T.kc2[:])
+    cp("ZT", "kTr LZ", T.ZT[:], T.kTr[:].indirect(T.LZ[:, 0:32]))
+    dmas("Y", [(T.Z[j::16, 0:256], T.ZT[j::16, 16 * (5 * j % 16):16 * (5 * j % 16) + 256]) for j in range(16)], "dsh", "Z", "ZT")
+    ts("rB", "rI", T.rB[:], T.rI[:], 4, None, SH)
+    ts("gI", "pI", T.gI[:], T.pI[:], 4, None, SH)
+    cp("gF", "gI", T.gF[:], T.gI[:])
+    cp("pF", "pI", T.pF[:], T.pI[:])
+    ts("MJ", "rJ xF", T.MJ[:], T.rJ[:], T.xF[:], None, A.is_equal)
+    ts("DB", "rB xF", T.DB[:], T.rB[:], T.xF[:], None, A.is_equal)
+    ts("BO", "rB gF", T.BO[:], T.rB[:, 0:128], T.gF[:], None, A.is_equal)
+    ts("BOh", "BO", T.BOh[:], T.BO[:], 0.5, None, A.mult)
+    ts("BO32", "BO", T.BO32[:], T.BO[:], 32.0, None, A.mult)
+    ts("ID", "rI pF", T.ID[:], T.rI[:, 0:128], T.pF[:], None, A.is_equal)
+    ts("IDf", "rI pF", T.IDf[:], T.rI[:, 0:128], T.pF[:], None, A.is_equal)
+    ts("ID64", "ID", T.ID64[:], T.ID[:], 64.0, None, A.mult)
+    ts("SelC", "rJ xF", T.SelC[:], T.rJ[:, 0:128], T.xF[:], 16.0, A.is_equal, A.mult)
+    ts("colD", "gF", T.colD[:], T.gF[:], 16.0, 15.0, A.mult, A.add)
+    ts("QJ", "rI colD", T.QJ[:], T.rI[:, 0:144], T.colD[:], 1024.0, A.is_equal, A.mult)
+    ts("TIE", "rB", T.TIE[:], T.rB[:], -64.0, 960.0, A.mult, A.add)
+    ts("LM", "rI colC", T.LM[:], T.rI[:, 0:16], T.colC[:], None, A.add)
+    ts("lane", "rI xF", T.lane[:], T.rI[:, 0:16], 16.0, T.xF[:], A.mult, A.add)
+    ts("dm", "lane", T.dm[:], T.lane[:], float(W), None, A.add)
+    cp("riF", "rI", T.riF[:], T.rI[:])
+    ts("D0", "rJ", T.D0[:, 0:256], T.rJ[:], 0.0, None, A.is_gt)
+    ts("D0", "rJ", T.D0[:, 256:512], T.rJ[:], 0.0, None, A.is_gt)
+    LB = math.log(BASE)
+    fill("eb", T.eb[:, 0:1], 71.0)
+    fill("eb", T.eb[:, 1:2], 71.0 + math.log(2.53))
+    fill("eb", T.eb[:, 2:3], -48.0 * math.log(2.0))
+    act("wcol", "lane eb", T.wcol[:], T.lane[:], F.Exp, bias=T.eb[:, 0:1], scale=-LB)
+    act("THR", "riF eb", T.THR[:], T.riF[:], F.Exp, bias=T.eb[:, 1:2], scale=-LB)
+    fill("Ed", T.E[:, W:WD], 0.0)
+    fill("Kd", T.K[:, W:WD], 0.0)
+    fill("mv", T.mv[:], 0.0)
+    ts("CU", "rI xF", T.CU[:, 0:RO + 1], T.rI[:, 0:RO + 1], 16.0, T.xF[:], A.mult, A.add)
+    ts("Rt", "rI xF", T.Rt[:, 0:RO], T.rI[:, 0:RO], T.xF[:], 1000.0, A.is_equal, A.mult)
+    ts("Rt", "Rt", T.Rt[:, 0:RO], T.Rt[:, 0:RO], -1000.0, None, A.add)
+    ts("Dlt", "DB", T.Dlt[:], T.DB[:], 1000.0, -1000.0, A.mult, A.add)
+    ts("NB", "DB", T.NB[:], T.DB[:], -1e20, 1e20, A.mult, A.add)
+    for i in range(2):
+        a, b = 1536 * i, 1536 * (i + 1)
+        act("E", "recs%d eb" % i, T.E[:, a:b], T.recs[:, a:b], F.Exp, bias=T.eb[:, 2:3], scale=6.0 * math.log(2.0))
+    for i in range(4):
+        a, b = 768 * i, 768 * (i + 1)
+        cp("K", "kinI%d" % i, T.K[:, a:b], T.kinI[:, a:b])
+
+    def late_constants():
+        tt("THJ", "THR MJ", T.THJ[:], T.THR[:], T.MJ[:], A.mult)
+        ts("tq", "MJ", T.tq[:], T.MJ[:], -1.0, None, A.add)
+        tt("THJ", "THJ tq", T.THJ[:], T.THJ[:], T.tq[:], A.add)
+        for t in range(RO):
+            ts("tq", "DB", T.tq[:], T.DB[:], 0.9 * 64.0 ** (t - 3), None, A.mult)
+            tt("DT%d" % t, "tq NB", T.DT[:, 256 * t:256 * t + 256], T.tq[:], T.NB[:], A.max)
+
+    def remote(dst, out, in_, rs, r, w):
+        eng = topo.engines(core, dst)[::2]
+        m = 0
+        for e in eng:
+            m |= 1 << e
+        rid, pid, _ = topo.addr(dst)
+        dep("G", r.split(), w.split())
+        g.remote_dma(out, in_, sem[rs], sem.ls, pid, rid, m)
+        cnt["ls"] = cnt.get("ls", 0) + len(eng)
+        return len(eng)
+
+    def draw(t):
+        c = T.cTu[:, 16 * t:16 * t + 16]
+        cp("cTu%d" % t, "Z offs", c, T.Z[:, 0:256].indirect(T.offs[:, 0:1]))
+        cp("cT2a", "cTu%d" % t, T.cT2[:, 0:32:2], c)
+        cp("cT2b", "cTu%d" % t, T.cT2[:, 1:32:2], c)
+        f = ("cTf", T.cTf) if t % 2 == 0 else ("cTg", T.cTg)
+        cp(f[0], "Z offs", f[1][:], T.Z[:, 0:256].indirect(T.offs[:, 0:1]))
+
+    draw(0)
+    ident = T.ID[:]
+    Ew, Kw, Ww, Iw = T.E[:, 0:W], T.K[:, 0:W], T.Wt[:], T.IOTA[:]
+    NP = 4
+    for t in range(RO):
+        TT = 8 + t
+        asked = T.cores[(rank + 1 + t % 3) % 4]
+        asker = T.cores[(rank - 1 - t % 3) % 4]
+        cu = T.cTu[:, 16 * t:16 * t + 16]
+        cuk = "cTu%d" % t
+        cfk, cf = ("cTf", T.cTf) if t % 2 == 0 else ("cTg", T.cTg)
+        last = t == RO - 1
+        ne = remote(asked, T.ql[:, 16 * t:16 * t + 16], cu, "qa%d" % t, cuk, "")
+        lastw["ql%d" % t] = ("qa%d" % t, ne)
+        lastw["rl%d" % t] = ("ra%d" % t, ne)
+        cp("kcu", "K Kd " + cuk, T.kcu[:], Kw.indirect(cu))
+        act("kc2", "K Kd cT2a cT2b", T.kc2[:], Kw.indirect(T.cT2[:, 0:32]), F.Copy)
+        if t > 0:
+            tt("E Ed", "Ec iT SL", T.E[:].indirect(T.SL[:]), T.Ec[:], T.iT[:], A.add)
+        act("wc", "Wt " + cuk, T.wc[:], Ww.indirect(cu), F.Copy)
+        act("Ec", "E " + cuk, T.Ec[:], Ew.indirect(cu), F.Copy)
+        mm("pES", "Ec ID", T.pES[:, 0:256], ident, T.Ec[:], True, False)
+        cp("cbu", "IOTA " + cuk, T.cbu[:], Iw.indirect(cu))
+
+        def own(k):
+            a, b = 1024 * k, 1024 * (k + 1)
+            act("GE%d" % k, "E kcu", T.GE[:, a:b], Ew.indirect(T.kcu[:, 64 * k:64 * k + 64]), F.Copy)
+
+        def own_sum(k):
+            a, b = 1024 * k, 1024 * (k + 1)
+            for m in range(16):
+                mm("pES", "GE%d ID" % k, T.pES[:, 64 * k:64 * k + 64], ident, T.GE[:, a + m:b:16], False, False)
+
+        def foreign(k):
+            a, b = 1024 * k, 1024 * (k + 1)
+            act("FE%d" % k, "E fku", T.FE[:, a:b], Ew.indirect(T.fku[:, 64 * k:64 * k + 64]), F.Copy)
+
+        def foreign_sum(k):
+            a, b = 1024 * k, 1024 * (k + 1)
+            for m in range(16):
+                mm("pFS", "FE%d ID" % k, T.pFS[:, 64 * k:64 * k + 64], ident, T.FE[:, a + m:b:16], m == 0, m == 15)
+        own(0)
+        vtr("kTr", "kc2", T.kTr[:], T.kc2[:])
+        cp("kTu", "kTr LZ", T.kTu[:], T.kTr[:].indirect(T.LZ[:, 0:16]))
+        own(1)
+        cp("fku", "K Kd ql%d" % t, T.fku[:], Kw.indirect(T.ql[:, 16 * t:16 * t + 16]))
+        for k in range(NP):
+            foreign(k)
+        for m in range(16):
+            tt("X%d" % m, "Wt kTu wc", T.X[:, 256 * m:256 * m + 256], Ww.indirect(T.kTu[:, 16 * m:16 * m + 16]), T.wc[:], A.max)
+        cp("kTi", "kTr LQ", T.kTi[:], T.kTr[:].indirect(T.LQ[:]))
+        ts("hi", "kTi", T.hi[:], T.kTi[:], 6, None, SH)
+        ts("lo", "kTi", T.lo[:], T.kTi[:], 63, None, AND)
+        if t == 0:
+            late_constants()
+        own(2)
+        for k in range(2):
+            own_sum(k)
+        for k in range(NP):
+            foreign_sum(k)
+        fs = T.fs[:, 256 * t:256 * t + 256]
+        act("fs%d" % t, "pFS", fs, T.pFS[:, 0:256], F.Copy)
+        ne = remote(asker, T.rl[:, 256 * t:256 * t + 256], fs, "ra%d" % t, "fs%d" % t, "")
+        own(3)
+        if not last:
+            act("kcf", "K Kd " + cuk, T.kcf[:], Kw.indirect(cu), F.Copy)
+            act("cbf", "IOTA " + cuk, T.cbf[:], Iw.indirect(cu), F.Copy)
+        mm("pS1", "TIE ID", T.pS1[:, 0:256], ident, T.TIE[:], True, False)
+        xs = " ".join("X%d" % m for m in range(16))
+        for j in range(16):
+            mm("pS1", xs + " QJ", T.pS1[:, 0:256], T.QJ[:, 15 - j:143 - j], T.X[:, j::16], False, j == 15)
+        act("S1s", "pS1", T.S1s[:], T.pS1[:, 0:256], F.Copy)
+        for b in range(16):
+            o, n = XB[b], 256 - 16 * b
+            ts("EQT%d" % b, "cbu wcol " + cfk, T.EQT[:, o:o + n], T.cbu[:, 16 * b:256], cf[:, b:b + 1], T.wcol[:, b:b + 1], A.is_equal, A.mult)
+            mm("pEQ", "EQT%d BO" % b, T.pEQ[:, 16 * b:256], T.BO[:], T.EQT[:, o:o + n], b == 0, b == 15)
+        tt("kHLa", "S1s LM hi", T.kHL[:, 0:256], T.S1s[:].indirect(T.LM[:]), T.hi[:], A.add)
+        tt("kHLb", "S1s LM lo", T.kHL[:, 256:512], T.S1s[:].indirect(T.LM[:]), T.lo[:], A.add)
+        tt("dupb", "pEQ THR", T.dupb[:], T.pEQ[:, 0:256], T.THR[:], A.is_ge)
+        tt("MJc", "pEQ THJ", T.MJc[:], T.pEQ[:, 0:256], T.THJ[:], A.is_lt)
+        scanmax("sHL", "kHLa kHLb", T.sHL[:], T.kHL[:])
+        scan("cs", "MJc", T.cs[:], T.MJc[:])
+        tt("sl1", "dm " + cfk, T.sl1[:], cf[:], T.dm[:], A.subtract)
+        cp("bI", "sHL", T.bI[:], T.sHL[:, 15:512:16])
+        tt("sl2", "sl1 cs", T.sl2[:], T.sl1[:], T.cs[:, 15:256:16], A.mult)
+        ts("bI2", "bI", T.bI2[:], T.bI[:], 63, None, AND)
+        tt("sl1", "sl2 dm", T.sl1[:], T.sl2[:], T.dm[:], A.add)
+        ts("b64", "bI2", T.b64[:], T.bI2[:, 0:16], 64.0, None, A.mult)
+        cp("SL", "sl1", T.SL[:], T.sl1[:])
+        tt("best", "b64 bI2", T.best[:], T.b64[:], T.bI2[:, 16:32], A.add)
+        if not last:
+            tt("kda", "cbf kcf", T.kd[:, 0:256:2], T.cbf[:, 1:256:2], T.kcf[:, 0:256:2], A.subtract)
+            tt("kdb", "cbf kcf", T.kd[:, 1:256:2], T.cbf[:, 0:256:2], T.kcf[:, 1:256:2], A.subtract)
+        tt("db", "best " + cfk, T.db[:], T.best[:], cf[:], A.subtract)
+        tt("dp", "best " + cfk, T.dp[:, 0:15], cf[:, 0:15], T.best[:, 1:16], A.subtract)
+        for k in range(2, NP):
+            own_sum(k)
+        mm("pZ", "dupb ID64", T.pZ[:, 0:256], T.ID64[:], T.dupb[:], True, False)
+        if not last:
+            mm("pU", "CU IDf", T.pU[:, 0:1], T.IDf[:], T.CU[:, t + 1:t + 2], True, False)
+        mm("pES", "rl%d ID" % t, T.pES[:, 0:256], ident, T.rl[:, 256 * t:256 * t + 256], False, True)
+        ts("X1", "pES", T.X1[:], T.pES[:, 0:256], 0.9 * 64.0 ** (t - 2), 0.5, A.is_ge, A.subtract)
+        tt("X2", "pES DT%d" % t, T.X2[:], T.pES[:, 0:256], T.DT[:, 256 * t:256 * t + 256], A.is_ge)
+        mm("pZ", "X1 BO", T.pZ[:, 0:256], T.BO[:], T.X1[:], False, False)
+        mm("pZ", "X2 BO32", T.pZ[:, 0:256], T.BO32[:], T.X2[:], False, True)
+        tt("iD", "pZ Dlt", T.iD[:], T.pZ[:, 0:256], T.Dlt[:], A.is_lt)
+        act("iT", "iD", T.iT[:], T.iD[:], F.Copy, scale=64.0 ** t)
+        if not last:
+            op("V", lambda: g.vector.tensor_reduce(T.cn[:], T.iD[:], AxisListType.X, A.add), "cn", "iD")
+            mm("pU", "cn SelC", T.pU[:, 0:1], T.SelC[:], T.cn[:], False, True)
+        tt("qm", "pZ MJc", T.qm[:], T.pZ[:, 0:256], T.MJc[:], A.mult)
+        scan("zs", "qm", T.zs[:], T.qm[:])
+        ze = T.zs[:, 15:256:16]
+        ts("z4", "zs", T.z4[:], ze, -4.0, None, A.add)
+        ts("a1", "zs", T.a1[:], ze, 0.0, None, A.is_lt)
+        ts("zy", "z4", T.zy[:], T.z4[:], 31, None, AND)
+        ts("od", "z4", T.od[:], T.z4[:], 1, None, AND)
+        ts("b3", "zy", T.b3[:], T.zy[:], 5.0, None, A.is_lt)
+        tt("tn", "a1 b3", T.tn[:], T.a1[:], T.b3[:], A.add)
+        tt("mv0", "od tn", T.mv0[:], T.od[:], T.tn[:], A.is_gt)
+        tt("mv", "mv0 tn", T.mv[:, 0:15], T.mv0[:, 0:15], T.tn[:, 1:16], A.mult)
+        tt("tm", "mv tn", T.tm[:], T.tn[:], T.mv[:], A.add)
+        tt("v1", "mv dp", T.v1[:, 0:15], T.mv[:, 0:15], T.dp[:, 0:15], A.mult)
+        tt("u1", "tm db", T.u1[:], T.tm[:], T.db[:], A.mult)
+        tt("nT", "u1 " + cfk, T.nT[:], T.u1[:], cf[:], A.add)
+        tt("nT", "nT v1", T.nT[:, 1:16], T.nT[:, 1:16], T.v1[:, 0:15], A.add)
+        cp("Z", "nT offs", T.Z[:, 0:256].indirect(T.offs[:, 0:1]), T.nT[:])
+        if not last:
+            ts("uk", "pU", T.uk[:], T.pU[:, 0:1], 1.0 / 256.0, -127.5 / 256.0, A.mult, A.add)
+            ts("offs", "uk pU", T.offs[:, 0:1], T.uk[:], -256.0, T.pU[:, 0:1], A.mult, A.add)
+            draw(t + 1)
+            ts("iR", "pZ Rt", T.iR[:], T.pZ[:, 0:256], T.Rt[:, t:t + 1], None, A.is_lt)
+            tt("kd2", "iR kda kdb", T.kd2[:], T.iR[:], T.kd[:], A.mult)
+            tt("K Kd", "kcf kd2 SL", T.K[:].indirect(T.SL[:]), T.kcf[:], T.kd2[:], A.add)
+
+    cp("Z2", "Z", T.Z[:, 256:512], T.Z[:, 0:256])
+    dmas("Y", [(T.ZT[j::16, 0:256], T.Z[j::16, 16 * (-5 * j % 16):16 * (-5 * j % 16) + 256]) for j in range(16)], "dun", "ZT", "Z Z2")
+    tt("E Ed", "Ec iT SL", T.E[:].indirect(T.SL[:]), T.Ec[:], T.iT[:], A.add)
+    for i in range(4):
+        a, b = 768 * i, 768 * (i + 1)
+        act("LN%d" % i, "E", T.LN[:, a:b], T.E[:, a:b], F.Ln)
+        ts("YR%d" % i, "LN%d" % i, T.YR[:, a:b], T.LN[:, a:b], 1.0 / (6.0 * math.log(2.0)), 136.0, A.mult, A.add)
+        ts("YQ%d" % i, "YR%d" % i, T.YR2[:, a:b], T.YR[:, a:b], -128.0, None, A.add)
+        dmas("Y", [(T.yr[:, a:b], T.YR2[:, a:b])], "dy%d" % i, "", "YQ%d" % i)
+    cp("kc2", "ZT L2", T.kc2[:], T.ZT[:, 0:256].indirect(T.L2[:, 0:32]))
+    vtr("kTr", "kc2", T.kTr[:], T.kc2[:])
+    cp("ysb", "kTr LQ", T.ysb[:], T.kTr[:].indirect(T.LQ[:]))
+    dmas("Y", [(T.ys[:], T.ysb[:])], "dys", "", "ysb")
+    for s in cnt:
+        if clock["G"].get(s, 0) < cnt[s]:
+            g.wait_ge(sem[s], cnt[s])

@@ -4,57 +4,52 @@ from concourse.mybir import ActivationFunctionType as F
 from concourse.mybir import AxisListType
 
 RO = 6
+EQ1 = 6
+NV = 32
 W = 3072
 WD = W + 256
 BASE = 1.75
 XB = [256 * b - 8 * b * (b - 1) for b in range(17)]
 
-SCRATCH = {
-    "recs": ("sbuf", [128, W], "bfloat16"), "kinI": ("sbuf", [128, W], "int32"), "slI": ("sbuf", [128, 256], "int32"),
-    "E": ("sbuf", [128, WD], "bfloat16"), "K": ("sbuf", [128, WD], "float32"), "Wt": ("sbuf", [128, W], "bfloat16"),
-    "IOTA": ("sbuf", [128, W], "float32"), "LN": ("sbuf", [128, W], "float32"),
-    "YR": ("sbuf", [128, W], "bfloat16"), "YR2": ("sbuf", [128, W], "bfloat16"),
-    "GE": ("sbuf", [128, 4096], "bfloat16"), "FE": ("sbuf", [128, 4096], "bfloat16"), "X": ("sbuf", [128, 4096], "bfloat16"), "S1s": ("sbuf", [128, 256], "float32"), "LM": ("sbuf", [128, 16], "uint16"),
-    "Z": ("sbuf", [128, 512], "float32"), "ZT": ("sbuf", [128, 512], "float32"), "ysb": ("sbuf", [128, 256], "float32"),
-    "kc2": ("sbuf", [128, 512], "float32"), "kTr": ("sbuf", [128, 512], "float32"),
-    "kcu": ("sbuf", [128, 256], "uint16"), "fku": ("sbuf", [128, 256], "uint16"), "kTu": ("sbuf", [128, 256], "uint16"),
-    "kTi": ("sbuf", [128, 256], "int32"), "hi": ("sbuf", [128, 256], "int32"), "lo": ("sbuf", [128, 256], "int32"),
-    "kHL": ("sbuf", [128, 512], "float32"), "sHL": ("sbuf", [128, 512], "float32"),
-    "bI": ("sbuf", [128, 32], "int32"), "bI2": ("sbuf", [128, 32], "int32"), "b64": ("sbuf", [128, 16], "float32"),
-    "best": ("sbuf", [128, 16], "float32"), "db": ("sbuf", [128, 16], "float32"), "dp": ("sbuf", [128, 16], "float32"),
-    "cT2": ("sbuf", [128, 32], "uint16"), "cTf": ("sbuf", [128, 16], "float32"), "cTg": ("sbuf", [128, 16], "float32"),
-    "cbu": ("sbuf", [128, 256], "uint16"), "cbf": ("sbuf", [128, 256], "float32"), "kcf": ("sbuf", [128, 256], "float32"),
-    "kd": ("sbuf", [128, 256], "float32"), "kd2": ("sbuf", [128, 256], "float32"), "iR": ("sbuf", [128, 256], "float32"),
-    "Ec": ("sbuf", [128, 256], "bfloat16"), "wc": ("sbuf", [128, 256], "bfloat16"),
-    "EQT": ("sbuf", [128, XB[16]], "bfloat16"), "dupb": ("sbuf", [128, 256], "bfloat16"),
-    "MJc": ("sbuf", [128, 256], "float32"), "cs": ("sbuf", [128, 256], "float32"),
-    "sl1": ("sbuf", [128, 16], "float32"), "sl2": ("sbuf", [128, 16], "float32"), "SL": ("sbuf", [128, 16], "uint16"),
-    "X1": ("sbuf", [128, 256], "bfloat16"), "X2": ("sbuf", [128, 256], "bfloat16"),
-    "iD": ("sbuf", [128, 256], "bfloat16"), "iT": ("sbuf", [128, 256], "bfloat16"), "cn": ("sbuf", [128, 1], "float32"),
-    "qm": ("sbuf", [128, 256], "float32"), "zs": ("sbuf", [128, 256], "float32"),
-    "z4": ("sbuf", [128, 16], "int32"), "zy": ("sbuf", [128, 16], "int32"), "od": ("sbuf", [128, 16], "int32"),
-    "a1": ("sbuf", [128, 16], "float32"), "b3": ("sbuf", [128, 16], "float32"), "tn": ("sbuf", [128, 16], "float32"),
-    "mv0": ("sbuf", [128, 16], "float32"), "mv": ("sbuf", [128, 16], "float32"), "tm": ("sbuf", [128, 16], "float32"),
-    "u1": ("sbuf", [128, 16], "float32"), "v1": ("sbuf", [128, 16], "float32"), "nT": ("sbuf", [128, 16], "float32"),
-    "uk": ("sbuf", [128, 1], "int32"), "offs": ("sbuf", [128, 2], "uint16"),
-    "pI": ("sbuf", [128, 1], "int32"), "pF": ("sbuf", [128, 1], "float32"), "xI": ("sbuf", [128, 1], "int32"), "xF": ("sbuf", [128, 1], "float32"),
-    "gI": ("sbuf", [128, 1], "int32"), "gF": ("sbuf", [128, 1], "float32"), "hI": ("sbuf", [128, 1], "int32"), "hF": ("sbuf", [128, 1], "float32"),
-    "colA": ("sbuf", [128, 1], "float32"), "colB": ("sbuf", [128, 1], "float32"), "colC": ("sbuf", [128, 1], "float32"), "colD": ("sbuf", [128, 1], "float32"),
-    "rI": ("sbuf", [128, 256], "int32"), "rJ": ("sbuf", [128, 256], "int32"), "rB": ("sbuf", [128, 256], "int32"), "rH": ("sbuf", [128, 32], "int32"),
-    "MJ": ("sbuf", [128, 256], "float32"), "DB": ("sbuf", [128, 256], "float32"), "NB": ("sbuf", [128, 256], "float32"), "tq": ("sbuf", [128, 256], "float32"),
-    "BO": ("sbuf", [128, 128], "bfloat16"), "BOh": ("sbuf", [128, 128], "bfloat16"), "BO32": ("sbuf", [128, 128], "bfloat16"),
-    "ID": ("sbuf", [128, 128], "bfloat16"), "ID64": ("sbuf", [128, 128], "bfloat16"), "IDf": ("sbuf", [128, 128], "float32"), "SelC": ("sbuf", [128, 128], "float32"),
-    "QJ": ("sbuf", [128, 144], "bfloat16"), "TIE": ("sbuf", [128, 256], "bfloat16"),
-    "lane": ("sbuf", [128, 16], "float32"), "dm": ("sbuf", [128, 16], "float32"), "wcol": ("sbuf", [128, 16], "float32"),
-    "riF": ("sbuf", [128, 256], "float32"), "THR": ("sbuf", [128, 256], "float32"), "THJ": ("sbuf", [128, 256], "float32"),
-    "DT": ("sbuf", [128, RO * 256], "bfloat16"), "Dlt": ("sbuf", [128, 256], "float32"), "Rt": ("sbuf", [128, 8], "float32"), "CU": ("sbuf", [128, 8], "float32"),
-    "eb": ("sbuf", [128, 4], "float32"),
-    "D0": ("sbuf", [128, 512], "float32"), "L1": ("sbuf", [128, 32], "uint16"), "L2": ("sbuf", [128, 32], "uint16"), "LZ": ("sbuf", [128, 32], "uint16"), "LQ": ("sbuf", [128, 16], "uint16"),
-    "cTu": ("sbuf", [128, 16 * RO], "uint16"), "ql": ("sbuf", [128, 16 * RO], "uint16"),
-    "fs": ("sbuf", [128, 256 * RO], "bfloat16"), "rl": ("sbuf", [128, 256 * RO], "bfloat16"),
-    "pES": ("psum", [128, 512], "float32"), "pFS": ("psum", [128, 512], "float32"), "pEQ": ("psum", [128, 512], "float32"),
-    "pS1": ("psum", [128, 512], "float32"), "pZ": ("psum", [128, 512], "float32"), "pU": ("psum", [128, 512], "float32"),
-}
+SCRATCH = {}
+
+
+def _bufs(where, n, dtype, names):
+    for k in names.split():
+        SCRATCH[k] = (where, [128, n], dtype)
+
+
+_bufs("sbuf", W, "bfloat16", "recs Wt")
+_bufs("sbuf", W, "int32", "kinI")
+_bufs("sbuf", W, "float32", "IOTA")
+_bufs("sbuf", WD, "bfloat16", "E")
+_bufs("sbuf", WD, "float32", "K")
+_bufs("sbuf", 4096, "bfloat16", "GE FE X")
+_bufs("sbuf", XB[16], "bfloat16", "EQT")
+_bufs("sbuf", 512, "float32", "Z ZT kc2 kTr D0")
+_bufs("sbuf", 256, "int32", "slI rI rJ rB")
+_bufs("sbuf", 256, "uint16", "kcu fku kTu cbu")
+_bufs("sbuf", 256, "float32", "kcf kcm cXm S1s S1p sH Pm MJc cs MJ DB THR THJ riF tq")
+_bufs("sbuf", 512, "bfloat16", "wc DT DBt")
+_bufs("sbuf", 256, "bfloat16", "Ec X1 X2 TIE")
+_bufs("sbuf", 16, "int32", "bI bI2 z4 zy od")
+_bufs("sbuf", 16, "uint16", "mu SL cTs LM LQ LP")
+_bufs("sbuf", 16, "float32", "db dp cTf cTg sl1 m1 m2 zc b3 tn mv0 mv tm u1 v1 nT lane dm wcol Dg OH")
+_bufs("sbuf", 16, "bfloat16", "a1")
+_bufs("sbuf", 32, "uint16", "L1 L2 LZ")
+_bufs("sbuf", 32, "int32", "rH")
+_bufs("sbuf", 32, "float32", "um")
+_bufs("sbuf", 128, "bfloat16", "BO ID ON")
+_bufs("sbuf", 128, "float32", "PX SW")
+_bufs("sbuf", 144, "bfloat16", "Q16 Q1 Q32")
+_bufs("sbuf", 144, "float32", "Q1f")
+_bufs("sbuf", 1, "int32", "pI xI gI hI oI uk")
+_bufs("sbuf", 1, "float32", "pF xF gF hF oF colA colB colC colD colE colF colG")
+_bufs("sbuf", 8, "float32", "eb Ne Nn")
+_bufs("sbuf", 2, "uint16", "of0 of1")
+_bufs("psum", 512, "float32", "pES pFS pEQ pS1 pZ pU pB pX")
+_bufs("sbuf", 16 * RO, "uint16", "cTu ql")
+_bufs("sbuf", 256 * RO, "bfloat16", "fs rl")
 SEMAPHORES = ["sv", "ss", "sp", "sg", "ls", "dsl", "dsh", "dun", "dys", "dw"] + ["dk%d" % i for i in range(4)] + ["dr%d" % i for i in range(2)] + ["dy%d" % i for i in range(4)] \
     + ["qa%d" % t for t in range(RO)] + ["ra%d" % t for t in range(RO)]
 
@@ -140,17 +135,13 @@ def rank_program(g, core, T, topo):
     def fill(w, ap, v):
         op("V", lambda: g.vector.memset(ap, v), w, "")
 
-    def scan(w, r, out, d1):
-        n = 256
-        op("V", lambda: g.vector.tensor_tensor_scan(out, T.D0[:, 0:n], d1, 0.0, A.mult, A.add), w, r + " D0")
-
-    def scanmax(w, r, out, d1):
-        op("V", lambda: g.vector.tensor_tensor_scan(out, T.D0[:], d1, 0.0, A.mult, A.max), w, r + " D0")
+    def scan(w, r, out, d1, o):
+        op("V", lambda: g.vector.tensor_tensor_scan(out, T.D0[:, 0:256], d1, 0.0, A.mult, o), w, r + " D0")
 
     def vtr(w, r, out, in_):
         op("V", lambda: g.vector.transpose(out, in_), w, r)
 
-    def act(w, r, out, in_, f, bias=0.0, scale=1.0):
+    def act(w, r, out, in_, f=F.Copy, bias=0.0, scale=1.0):
         op("S", lambda: g.scalar.activation(out, in_, f, bias=bias, scale=scale), w, r)
 
     def mm(w, r, out, l, x, st, sp):
@@ -162,81 +153,98 @@ def rank_program(g, core, T, topo):
         dmas("Y" if i < 2 else "S", [(T.kinI[:, a:b], T.kin[:, a:b])], "dk%d" % i, "kinI%d" % i, "")
     for i in range(2):
         a, b = 1536 * i, 1536 * (i + 1)
-        dmas("Y", [(T.recs[:, a:b], T.rec[:, a:b])], "dr%d" % i, "recs%d" % i, "")
+        dmas("Y" if i else "S", [(T.recs[:, a:b], T.rec[:, a:b])], "dr%d" % i, "recs%d" % i, "")
     dmas("S", [(T.Wt[:], T.wealth[:])], "dw", "Wt", "")
 
     op("G", lambda: g.iota(T.pI[:], [[0, 1]], 0, 1), "pI", "")
     op("G", lambda: g.iota(T.rI[:], [[1, 256]], 0, 0), "rI", "")
     op("G", lambda: g.iota(T.IOTA[:], [[1, W]], 0, 0, allow_small_or_imprecise_dtypes=True), "IOTA", "")
     SH, AND = A.arith_shift_right, A.bitwise_and
+    fill("eb", T.eb[:, 2:3], -48.0 * math.log(2.0))
     ts("xI", "pI", T.xI[:], T.pI[:], 15, None, AND)
     ts("hI", "pI", T.hI[:], T.pI[:], 16, None, AND)
     ts("rH", "rI", T.rH[:], T.rI[:, 0:32], 1, None, SH)
     ts("rJ", "rI", T.rJ[:], T.rI[:], 15, None, AND)
     cp("xF", "xI", T.xF[:], T.xI[:])
     cp("hF", "hI", T.hF[:], T.hI[:])
-    ts("colC", "xF", T.colC[:], T.xF[:], 16.0, None, A.mult)
     ts("colA", "xF hF", T.colA[:], T.xF[:], 32.0, T.hF[:], A.mult, A.add)
-    tt("colB", "xF hF", T.colB[:], T.xF[:], T.hF[:], A.add)
     ts("L1", "rH xF", T.L1[:], T.rH[:], 16.0, T.xF[:], A.mult, A.add)
     ts("LZ", "rJ colA", T.LZ[:], T.rJ[:, 0:32], T.colA[:], None, A.add)
-    ts("LQ", "rI colB", T.LQ[:], T.rI[:, 0:16], 32.0, T.colB[:], A.mult, A.add)
-    ts("L2", "rH colC", T.L2[:], T.rH[:], T.colC[:], None, A.add)
-    cp("offs", "xF", T.offs[:, 0:1], T.xF[:])
+    cp("of0", "xF", T.of0[:, 0:1], T.xF[:])
     cp("kc2", "slI L1", T.kc2[:], T.slI[:].indirect(T.L1[:, 0:32]))
-    vtr("kTr", "kc2", T.kTr[:], T.kc2[:])
-    cp("ZT", "kTr LZ", T.ZT[:], T.kTr[:].indirect(T.LZ[:, 0:32]))
+    vtr("kTa kTb", "kc2", T.kTr[:], T.kc2[:])
+    cp("ZT", "kTa kTb LZ", T.ZT[:], T.kTr[:].indirect(T.LZ[:, 0:32]))
     dmas("Y", [(T.Z[j::16, 0:256], T.ZT[j::16, 16 * (5 * j % 16):16 * (5 * j % 16) + 256]) for j in range(16)], "dsh", "Z", "ZT")
-    ts("rB", "rI", T.rB[:], T.rI[:], 4, None, SH)
-    ts("gI", "pI", T.gI[:], T.pI[:], 4, None, SH)
-    cp("gF", "gI", T.gF[:], T.gI[:])
-    cp("pF", "pI", T.pF[:], T.pI[:])
-    ts("MJ", "rJ xF", T.MJ[:], T.rJ[:], T.xF[:], None, A.is_equal)
-    ts("DB", "rB xF", T.DB[:], T.rB[:], T.xF[:], None, A.is_equal)
-    ts("BO", "rB gF", T.BO[:], T.rB[:, 0:128], T.gF[:], None, A.is_equal)
-    ts("BOh", "BO", T.BOh[:], T.BO[:], 0.5, None, A.mult)
-    ts("BO32", "BO", T.BO32[:], T.BO[:], 32.0, None, A.mult)
-    ts("ID", "rI pF", T.ID[:], T.rI[:, 0:128], T.pF[:], None, A.is_equal)
-    ts("IDf", "rI pF", T.IDf[:], T.rI[:, 0:128], T.pF[:], None, A.is_equal)
-    ts("ID64", "ID", T.ID64[:], T.ID[:], 64.0, None, A.mult)
-    ts("SelC", "rJ xF", T.SelC[:], T.rJ[:, 0:128], T.xF[:], 16.0, A.is_equal, A.mult)
-    ts("colD", "gF", T.colD[:], T.gF[:], 16.0, 15.0, A.mult, A.add)
-    ts("QJ", "rI colD", T.QJ[:], T.rI[:, 0:144], T.colD[:], 1024.0, A.is_equal, A.mult)
-    ts("TIE", "rB", T.TIE[:], T.rB[:], -64.0, 960.0, A.mult, A.add)
-    ts("LM", "rI colC", T.LM[:], T.rI[:, 0:16], T.colC[:], None, A.add)
-    ts("lane", "rI xF", T.lane[:], T.rI[:, 0:16], 16.0, T.xF[:], A.mult, A.add)
-    ts("dm", "lane", T.dm[:], T.lane[:], float(W), None, A.add)
-    cp("riF", "rI", T.riF[:], T.rI[:])
-    ts("D0", "rJ", T.D0[:, 0:256], T.rJ[:], 0.0, None, A.is_gt)
-    ts("D0", "rJ", T.D0[:, 256:512], T.rJ[:], 0.0, None, A.is_gt)
-    LB = math.log(BASE)
-    fill("eb", T.eb[:, 0:1], 71.0)
-    fill("eb", T.eb[:, 1:2], 71.0 + math.log(2.53))
-    fill("eb", T.eb[:, 2:3], -48.0 * math.log(2.0))
-    act("wcol", "lane eb", T.wcol[:], T.lane[:], F.Exp, bias=T.eb[:, 0:1], scale=-LB)
-    act("THR", "riF eb", T.THR[:], T.riF[:], F.Exp, bias=T.eb[:, 1:2], scale=-LB)
     fill("Ed", T.E[:, W:WD], 0.0)
     fill("Kd", T.K[:, W:WD], 0.0)
-    fill("mv", T.mv[:], 0.0)
-    ts("CU", "rI xF", T.CU[:, 0:RO + 1], T.rI[:, 0:RO + 1], 16.0, T.xF[:], A.mult, A.add)
-    ts("Rt", "rI xF", T.Rt[:, 0:RO], T.rI[:, 0:RO], T.xF[:], 1000.0, A.is_equal, A.mult)
-    ts("Rt", "Rt", T.Rt[:, 0:RO], T.Rt[:, 0:RO], -1000.0, None, A.add)
-    ts("Dlt", "DB", T.Dlt[:], T.DB[:], 1000.0, -1000.0, A.mult, A.add)
-    ts("NB", "DB", T.NB[:], T.DB[:], -1e20, 1e20, A.mult, A.add)
+    ts("rB", "rI", T.rB[:], T.rI[:], 4, None, SH)
+    ts("gI", "pI", T.gI[:], T.pI[:], 4, None, SH)
+    cp("pF", "pI", T.pF[:], T.pI[:])
+    cp("gF", "gI", T.gF[:], T.gI[:])
+    ts("ID", "rI pF", T.ID[:], T.rI[:, 0:128], T.pF[:], None, A.is_equal)
     for i in range(2):
         a, b = 1536 * i, 1536 * (i + 1)
         act("E", "recs%d eb" % i, T.E[:, a:b], T.recs[:, a:b], F.Exp, bias=T.eb[:, 2:3], scale=6.0 * math.log(2.0))
     for i in range(4):
         a, b = 768 * i, 768 * (i + 1)
-        cp("K", "kinI%d" % i, T.K[:, a:b], T.kinI[:, a:b])
+        cp("K%d" % i, "kinI%d" % i, T.K[:, a:b], T.kinI[:, a:b])
+    KK = "K0 K1 K2 K3 Kd"
+    LB = math.log(BASE)
+
+    def swap_constants():
+        ts("colG", "hF pF", T.colG[:], T.hF[:], -2.0, T.pF[:], A.mult, A.add)
+        ts("colG", "colG", T.colG[:], T.colG[:], 16.0, None, A.add)
+        ts("SW", "rI colG", T.SW[:], T.rI[:, 0:128], T.colG[:], None, A.is_equal)
+        ts("oI", "pI", T.oI[:], T.pI[:], 1, None, AND)
+        cp("oF", "oI", T.oF[:], T.oI[:])
+        ts("gI", "hI", T.gI[:], T.hI[:], 4, None, SH)
+        tt("colF", "oF gI", T.colF[:], T.oF[:], T.gI[:], A.not_equal)
+        ts("xI", "xI", T.xI[:], T.xI[:], 1, None, SH)
+        ts("colE", "xI hF", T.colE[:], T.xI[:], 32.0, T.hF[:], A.mult, A.add)
+        ts("colF", "colF colE", T.colF[:], T.colF[:], 256.0, T.colE[:], A.mult, A.add)
+        ts("LP", "rI colF", T.LP[:], T.rI[:, 0:16], T.colF[:], None, A.add)
 
     def late_constants():
+        ts("colC", "xF", T.colC[:], T.xF[:], 16.0, None, A.mult)
+        ts("colD", "gF", T.colD[:], T.gF[:], 16.0, 15.0, A.mult, A.add)
+        tt("colB", "xF hF", T.colB[:], T.xF[:], T.hF[:], A.add)
+        ts("lane", "rI xF", T.lane[:], T.rI[:, 0:16], 16.0, T.xF[:], A.mult, A.add)
+        fill("eb0", T.eb[:, 0:1], 71.0)
+        fill("eb1", T.eb[:, 1:2], 71.0 + math.log(2.53))
+        cp("riF", "rI", T.riF[:], T.rI[:])
+        act("wcol", "lane eb0", T.wcol[:], T.lane[:], F.Exp, bias=T.eb[:, 0:1], scale=-LB)
+        act("THR", "riF eb1", T.THR[:], T.riF[:], F.Exp, bias=T.eb[:, 1:2], scale=-LB)
+        ts("Q16", "rI colD", T.Q16[:], T.rI[:, 0:144], T.colD[:], 16.0, A.is_equal, A.mult)
+        ts("Q1", "rI colD", T.Q1[:], T.rI[:, 0:144], T.colD[:], None, A.is_equal)
+        ts("Q32", "rI colD", T.Q32[:], T.rI[:, 0:144], T.colD[:], 32.0, A.is_equal, A.mult)
+        ts("Q1f", "rI colD", T.Q1f[:], T.rI[:, 0:144], T.colD[:], None, A.is_equal)
+        ts("BO", "rB gF", T.BO[:], T.rB[:, 0:128], T.gF[:], None, A.is_equal)
+        ts("TIE", "rB", T.TIE[:], T.rB[:], -1.0, 15.0, A.mult, A.add)
+        ts("LM", "rI colC", T.LM[:], T.rI[:, 0:16], T.colC[:], None, A.add)
+        ts("D0", "rJ", T.D0[:, 0:256], T.rJ[:], 0.0, None, A.is_gt)
+        ts("MJ", "rJ xF", T.MJ[:], T.rJ[:], T.xF[:], None, A.is_equal)
+        ts("DB", "rB xF", T.DB[:], T.rB[:], T.xF[:], None, A.is_equal)
+
+    def later_constants():
+        ts("dm", "lane", T.dm[:], T.lane[:], float(W), None, A.add)
         tt("THJ", "THR MJ", T.THJ[:], T.THR[:], T.MJ[:], A.mult)
         ts("tq", "MJ", T.tq[:], T.MJ[:], -1.0, None, A.add)
         tt("THJ", "THJ tq", T.THJ[:], T.THJ[:], T.tq[:], A.add)
-        for t in range(RO):
-            ts("tq", "DB", T.tq[:], T.DB[:], 0.9 * 64.0 ** (t - 3), None, A.mult)
-            tt("DT%d" % t, "tq NB", T.DT[:, 256 * t:256 * t + 256], T.tq[:], T.NB[:], A.max)
+        ts("riF", "DB THR", T.riF[:], T.DB[:], -1e20, 1e20, A.mult, A.add)
+        ts("tq", "DB", T.tq[:], T.DB[:], 0.9 * 64.0 ** -3, None, A.mult)
+        tt("DT0", "tq riF", T.DT[:, 0:256], T.tq[:], T.riF[:], A.max)
+        ts("colE", "xF", T.colE[:], T.xF[:], -1.0, 15.0, A.mult, A.add)
+        ts("OH", "rI colE", T.OH[:], T.rI[:, 0:16], T.colE[:], None, A.is_equal)
+        ts("colF", "oF pF", T.colF[:], T.oF[:], -2.0, T.pF[:], A.mult, A.add)
+        ts("colF", "colF", T.colF[:], T.colF[:], 1.0, None, A.add)
+        ts("PX", "rI colF", T.PX[:], T.rI[:, 0:128], T.colF[:], None, A.is_equal)
+        ts("Dg", "rI xF", T.Dg[:], T.rI[:, 0:16], T.xF[:], 16.0, A.is_equal, A.mult)
+        ts("Ne", "rI xF", T.Ne[:, 0:RO], T.rI[:, 0:RO], T.xF[:], None, A.is_equal)
+        ts("Nn", "rI xF", T.Nn[:, 0:RO], T.rI[:, 0:RO], T.xF[:], None, A.not_equal)
+        ts("LQ", "rI colB", T.LQ[:], T.rI[:, 0:16], 32.0, T.colB[:], A.mult, A.add)
+        ts("L2", "rH colC", T.L2[:], T.rH[:], T.colC[:], None, A.add)
+        fill("ON", T.ON[:], 1.0)
+        fill("mv", T.mv[:], 0.0)
 
     def remote(dst, out, in_, rs, r, w):
         eng = topo.engines(core, dst)[::2]
@@ -249,162 +257,182 @@ def rank_program(g, core, T, topo):
         cnt["ls"] = cnt.get("ls", 0) + len(eng)
         return len(eng)
 
-    def draw(t):
-        c = T.cTu[:, 16 * t:16 * t + 16]
-        cp("cTu%d" % t, "Z offs", c, T.Z[:, 0:256].indirect(T.offs[:, 0:1]))
-        cp("cT2a", "cTu%d" % t, T.cT2[:, 0:32:2], c)
-        cp("cT2b", "cTu%d" % t, T.cT2[:, 1:32:2], c)
-        f = ("cTf", T.cTf) if t % 2 == 0 else ("cTg", T.cTg)
-        cp(f[0], "Z offs", f[1][:], T.Z[:, 0:256].indirect(T.offs[:, 0:1]))
+    OF = (T.of0, T.of1)
 
-    draw(0)
+    def draw(t):
+        cp("cTu%d" % t, "Z of%d" % (t % 2), T.cTu[:, 16 * t:16 * t + 16], T.Z[:, 0:256].indirect(OF[t % 2][:, 0:1]))
+
+    def draw_more(t):
+        f = ("cTf", T.cTf) if t % 2 == 0 else ("cTg", T.cTg)
+        cp(f[0], "cTu%d" % t, f[1][:], T.cTu[:, 16 * t:16 * t + 16])
+
     ident = T.ID[:]
     Ew, Kw, Ww, Iw = T.E[:, 0:W], T.K[:, 0:W], T.Wt[:], T.IOTA[:]
-    NP = 4
+
+    def gather_e(eng, dst, dk, lst, lk, a, n):
+        out, in_ = dst[:, 16 * a:16 * (a + n)], Ew.indirect(lst[:, a:a + n])
+        if eng == "S":
+            act(dk, "E " + lk, out, in_)
+        else:
+            cp(dk, "E " + lk, out, in_)
+
+    def sum_e(ps, pk, dst, dk, a, n, st, sp):
+        for m in range(16):
+            mm(pk, dk + " ID", ps[:, a:a + n], ident, dst[:, 16 * a + m:16 * (a + n):16], st and m == 0, sp and m == 15)
+
+    draw(0)
     for t in range(RO):
-        TT = 8 + t
         asked = T.cores[(rank + 1 + t % 3) % 4]
         asker = T.cores[(rank - 1 - t % 3) % 4]
         cu = T.cTu[:, 16 * t:16 * t + 16]
         cuk = "cTu%d" % t
         cfk, cf = ("cTf", T.cTf) if t % 2 == 0 else ("cTg", T.cTg)
         last = t == RO - 1
+        dtk, dt_ = "DT%d" % (t % 2), T.DT[:, 256 * (t % 2):256 * (t % 2) + 256]
         ne = remote(asked, T.ql[:, 16 * t:16 * t + 16], cu, "qa%d" % t, cuk, "")
         lastw["ql%d" % t] = ("qa%d" % t, ne)
         lastw["rl%d" % t] = ("ra%d" % t, ne)
-        cp("kcu", "K Kd " + cuk, T.kcu[:], Kw.indirect(cu))
-        act("kc2", "K Kd cT2a cT2b", T.kc2[:], Kw.indirect(T.cT2[:, 0:32]), F.Copy)
+        cp("kcu", KK + " " + cuk, T.kcu[:], Kw.indirect(cu))
+        act("kcf", KK + " " + cuk, T.kcf[:], Kw.indirect(cu))
         if t > 0:
-            tt("E Ed", "Ec iT SL", T.E[:].indirect(T.SL[:]), T.Ec[:], T.iT[:], A.add)
-        act("wc", "Wt " + cuk, T.wc[:], Ww.indirect(cu), F.Copy)
-        act("Ec", "E " + cuk, T.Ec[:], Ew.indirect(cu), F.Copy)
-        mm("pES", "Ec ID", T.pES[:, 0:256], ident, T.Ec[:], True, False)
+            tt("E Ed", "Ec DBt SL", T.E[:].indirect(T.SL[:]), T.Ec[:], T.DBt[:, 0:256], A.add)
+        act("wc", "Wt " + cuk, T.wc[:, 0:256], Ww.indirect(cu))
+        act("wcb", "Wt " + cuk, T.wc[:, 256:512], Ww.indirect(cu))
+        act("Ec", "E " + cuk, T.Ec[:], Ew.indirect(cu))
+        vtr("kTa", "kcf", T.kTr[:, 0:256], T.kcf[:])
+        if t == 0:
+            swap_constants()
+        mm("pX", "kTa SW", T.pX[:, 0:256], T.SW[:], T.kTr[:, 0:256], True, True)
+        act("kTb", "pX", T.kTr[:, 256:512], T.pX[:, 0:256])
+        draw_more(t)
         cp("cbu", "IOTA " + cuk, T.cbu[:], Iw.indirect(cu))
-
-        def own(k):
-            a, b = 1024 * k, 1024 * (k + 1)
-            act("GE%d" % k, "E kcu", T.GE[:, a:b], Ew.indirect(T.kcu[:, 64 * k:64 * k + 64]), F.Copy)
-
-        def own_sum(k):
-            a, b = 1024 * k, 1024 * (k + 1)
-            for m in range(16):
-                mm("pES", "GE%d ID" % k, T.pES[:, 64 * k:64 * k + 64], ident, T.GE[:, a + m:b:16], False, False)
-
-        def foreign(k):
-            a, b = 1024 * k, 1024 * (k + 1)
-            act("FE%d" % k, "E fku", T.FE[:, a:b], Ew.indirect(T.fku[:, 64 * k:64 * k + 64]), F.Copy)
-
-        def foreign_sum(k):
-            a, b = 1024 * k, 1024 * (k + 1)
-            for m in range(16):
-                mm("pFS", "FE%d ID" % k, T.pFS[:, 64 * k:64 * k + 64], ident, T.FE[:, a + m:b:16], m == 0, m == 15)
-        own(0)
-        vtr("kTr", "kc2", T.kTr[:], T.kc2[:])
-        cp("kTu", "kTr LZ", T.kTu[:], T.kTr[:].indirect(T.LZ[:, 0:16]))
-        own(1)
-        cp("fku", "K Kd ql%d" % t, T.fku[:], Kw.indirect(T.ql[:, 16 * t:16 * t + 16]))
-        for k in range(NP):
-            foreign(k)
-        for m in range(16):
-            tt("X%d" % m, "Wt kTu wc", T.X[:, 256 * m:256 * m + 256], Ww.indirect(T.kTu[:, 16 * m:16 * m + 16]), T.wc[:], A.max)
-        cp("kTi", "kTr LQ", T.kTi[:], T.kTr[:].indirect(T.LQ[:]))
-        ts("hi", "kTi", T.hi[:], T.kTi[:], 6, None, SH)
-        ts("lo", "kTi", T.lo[:], T.kTi[:], 63, None, AND)
         if t == 0:
             late_constants()
-        own(2)
-        for k in range(2):
-            own_sum(k)
-        for k in range(NP):
-            foreign_sum(k)
-        fs = T.fs[:, 256 * t:256 * t + 256]
-        act("fs%d" % t, "pFS", fs, T.pFS[:, 0:256], F.Copy)
-        ne = remote(asker, T.rl[:, 256 * t:256 * t + 256], fs, "ra%d" % t, "fs%d" % t, "")
-        own(3)
-        if not last:
-            act("kcf", "K Kd " + cuk, T.kcf[:], Kw.indirect(cu), F.Copy)
-            act("cbf", "IOTA " + cuk, T.cbf[:], Iw.indirect(cu), F.Copy)
-        mm("pS1", "TIE ID", T.pS1[:, 0:256], ident, T.TIE[:], True, False)
-        xs = " ".join("X%d" % m for m in range(16))
-        for j in range(16):
-            mm("pS1", xs + " QJ", T.pS1[:, 0:256], T.QJ[:, 15 - j:143 - j], T.X[:, j::16], False, j == 15)
-        act("S1s", "pS1", T.S1s[:], T.pS1[:, 0:256], F.Copy)
-        for b in range(16):
+        gather_e("S", T.GE, "GE0", T.kcu, "kcu", 0, 64)
+        mm("pES", "Ec ID", T.pES[:, 0:256], ident, T.Ec[:], True, False)
+        sum_e(T.pES, "pES", T.GE, "GE0", 0, 64, False, False)
+
+        def equal(b):
             o, n = XB[b], 256 - 16 * b
             ts("EQT%d" % b, "cbu wcol " + cfk, T.EQT[:, o:o + n], T.cbu[:, 16 * b:256], cf[:, b:b + 1], T.wcol[:, b:b + 1], A.is_equal, A.mult)
+
+        def equal_sum(b):
+            o, n = XB[b], 256 - 16 * b
             mm("pEQ", "EQT%d BO" % b, T.pEQ[:, 16 * b:256], T.BO[:], T.EQT[:, o:o + n], b == 0, b == 15)
-        tt("kHLa", "S1s LM hi", T.kHL[:, 0:256], T.S1s[:].indirect(T.LM[:]), T.hi[:], A.add)
-        tt("kHLb", "S1s LM lo", T.kHL[:, 256:512], T.S1s[:].indirect(T.LM[:]), T.lo[:], A.add)
-        tt("dupb", "pEQ THR", T.dupb[:], T.pEQ[:, 0:256], T.THR[:], A.is_ge)
-        tt("MJc", "pEQ THJ", T.MJc[:], T.pEQ[:, 0:256], T.THJ[:], A.is_lt)
-        scanmax("sHL", "kHLa kHLb", T.sHL[:], T.kHL[:])
-        scan("cs", "MJc", T.cs[:], T.MJc[:])
+
+        def wealth(m):
+            tt("X%d" % m, "Wt kTu wc wcb", T.X[:, 512 * m:512 * m + 512], Ww.indirect(T.kTu[:, 32 * m:32 * m + 32]), T.wc[:], A.max)
+        for b in range(EQ1):
+            equal(b)
+        cp("kTu", "kTa kTb LP", T.kTu[:], T.kTr[:].indirect(T.LP[:]))
+        cp("fku", KK + " ql%d" % t, T.fku[:], Kw.indirect(T.ql[:, 16 * t:16 * t + 16]))
+        for m in range(8):
+            wealth(m)
+        for b in range(EQ1):
+            equal_sum(b)
+        for k in range(4):
+            gather_e("S", T.FE, "FE%d" % k, T.fku, "fku", 64 * k, 64)
+            sum_e(T.pFS, "pFS", T.FE, "FE%d" % k, 64 * k, 64, True, True)
+        gather_e("S", T.GE, "GE1", T.kcu, "kcu", 64, 32)
+        mm("pS1", "TIE ID", T.pS1[:, 0:256], ident, T.TIE[:], True, False)
+        xs = " ".join("X%d" % m for m in range(8))
+        for j in range(16):
+            mm("pS1", xs + " Q16", T.pS1[:, 0:256], T.Q16[:, 15 - j:143 - j], T.X[:, j::16], False, j == 15)
+        fs = T.fs[:, 256 * t:256 * t + 256]
+        act("fs%d" % t, "pFS", fs, T.pFS[:, 0:256])
+        remote(asker, T.rl[:, 256 * t:256 * t + 256], fs, "ra%d" % t, "fs%d" % t, "")
+        gather_e("S", T.GE, "GE1b", T.kcu, "kcu", 96, 32)
+        gather_e("S", T.GE, "GE2", T.kcu, "kcu", 128, 64)
+        act("S1s", "pS1", T.S1s[:], T.pS1[:, 0:256])
+        if NV < 64:
+            gather_e("S", T.GE, "GE3", T.kcu, "kcu", 192, 64 - NV)
+        if t == 0:
+            later_constants()
+        for b in range(EQ1, 16):
+            equal(b)
+            equal_sum(b)
+        sum_e(T.pES, "pES", T.GE, "GE1 GE1b", 64, 64, False, False)
         tt("sl1", "dm " + cfk, T.sl1[:], cf[:], T.dm[:], A.subtract)
-        cp("bI", "sHL", T.bI[:], T.sHL[:, 15:512:16])
-        tt("sl2", "sl1 cs", T.sl2[:], T.sl1[:], T.cs[:, 15:256:16], A.mult)
-        ts("bI2", "bI", T.bI2[:], T.bI[:], 63, None, AND)
-        tt("sl1", "sl2 dm", T.sl1[:], T.sl2[:], T.dm[:], A.add)
-        ts("b64", "bI2", T.b64[:], T.bI2[:, 0:16], 64.0, None, A.mult)
-        cp("SL", "sl1", T.SL[:], T.sl1[:])
-        tt("best", "b64 bI2", T.best[:], T.b64[:], T.bI2[:, 16:32], A.add)
         if not last:
-            tt("kda", "cbf kcf", T.kd[:, 0:256:2], T.cbf[:, 1:256:2], T.kcf[:, 0:256:2], A.subtract)
-            tt("kdb", "cbf kcf", T.kd[:, 1:256:2], T.cbf[:, 0:256:2], T.kcf[:, 1:256:2], A.subtract)
-        tt("db", "best " + cfk, T.db[:], T.best[:], cf[:], A.subtract)
-        tt("dp", "best " + cfk, T.dp[:, 0:15], cf[:, 0:15], T.best[:, 1:16], A.subtract)
-        for k in range(2, NP):
-            own_sum(k)
-        mm("pZ", "dupb ID64", T.pZ[:, 0:256], T.ID64[:], T.dupb[:], True, False)
+            mm("pX", "PX " + cfk, T.pX[:, 0:16], T.PX[:], cf[:], True, True)
+        gather_e("V", T.GE, "GE4", T.kcu, "kcu", 256 - NV, NV)
+        tt("MJc", "pEQ THJ", T.MJc[:], T.pEQ[:, 0:256], T.THJ[:], A.is_lt)
         if not last:
-            mm("pU", "CU IDf", T.pU[:, 0:1], T.IDf[:], T.CU[:, t + 1:t + 2], True, False)
+            cp("cTs", "pX", T.cTs[:], T.pX[:, 0:16])
+            ts("um1", "rI colC", T.um[:, 16:17], T.colC[:], 1.0 / 16.0, 16.0 * (t + 1), A.mult, A.add)
+        scan("cs", "MJc", T.cs[:], T.MJc[:], A.add)
+        sum_e(T.pES, "pES", T.GE, "GE2", 128, 64, False, False)
+        sum_e(T.pES, "pES", T.GE, "GE3 GE4", 192, 64, False, False)
         mm("pES", "rl%d ID" % t, T.pES[:, 0:256], ident, T.rl[:, 256 * t:256 * t + 256], False, True)
-        ts("X1", "pES", T.X1[:], T.pES[:, 0:256], 0.9 * 64.0 ** (t - 2), 0.5, A.is_ge, A.subtract)
-        tt("X2", "pES DT%d" % t, T.X2[:], T.pES[:, 0:256], T.DT[:, 256 * t:256 * t + 256], A.is_ge)
-        mm("pZ", "X1 BO", T.pZ[:, 0:256], T.BO[:], T.X1[:], False, False)
-        mm("pZ", "X2 BO32", T.pZ[:, 0:256], T.BO32[:], T.X2[:], False, True)
-        tt("iD", "pZ Dlt", T.iD[:], T.pZ[:, 0:256], T.Dlt[:], A.is_lt)
-        act("iT", "iD", T.iT[:], T.iD[:], F.Copy, scale=64.0 ** t)
+        cp("S1p", "S1s LM", T.S1p[:], T.S1s[:].indirect(T.LM[:]))
+        scan("sH", "S1p", T.sH[:], T.S1p[:], A.max)
         if not last:
-            op("V", lambda: g.vector.tensor_reduce(T.cn[:], T.iD[:], AxisListType.X, A.add), "cn", "iD")
-            mm("pU", "cn SelC", T.pU[:, 0:1], T.SelC[:], T.cn[:], False, True)
-        tt("qm", "pZ MJc", T.qm[:], T.pZ[:, 0:256], T.MJc[:], A.mult)
-        scan("zs", "qm", T.zs[:], T.qm[:])
-        ze = T.zs[:, 15:256:16]
-        ts("z4", "zs", T.z4[:], ze, -4.0, None, A.add)
-        ts("a1", "zs", T.a1[:], ze, 0.0, None, A.is_lt)
+            act("kcm", "kcf Nn", T.kcm[:], T.kcf[:], F.Copy, scale=T.Nn[:, t:t + 1])
+            act("cXm", "IOTA Ne cTs", T.cXm[:], Iw.indirect(T.cTs[:]), F.Copy, scale=T.Ne[:, t:t + 1])
+        act("DBt", "DB", T.DBt[:, 0:256], T.DB[:], F.Copy, scale=64.0 ** t)
+        if not last:
+            o = 256 * ((t + 1) % 2)
+            act("DT%d" % ((t + 1) % 2), dtk, T.DT[:, o:o + 256], dt_, F.Copy, scale=64.0)
+        ts("X1", "pES", T.X1[:], T.pES[:, 0:256], 0.9 * 64.0 ** (t - 2), 0.5, A.is_ge, A.subtract)
+        for j in range(16):
+            mm("pZ", "X1 Q1", T.pZ[:, 0:16], T.Q1[:, 15 - j:143 - j], T.X1[:, j::16], j == 0, False)
+        tt("X2", "pES " + dtk, T.X2[:], T.pES[:, 0:256], dt_, A.is_ge)
+        for j in range(16):
+            mm("pZ", "X2 Q32", T.pZ[:, 0:16], T.Q32[:, 15 - j:143 - j], T.X2[:, j::16], False, j == 15)
+        cp("bI", "sH", T.bI[:], T.sH[:, 15:256:16])
+        ts("bI2", "bI", T.bI2[:], T.bI[:], 15, None, AND)
+        cp("mu", "bI2", T.mu[:], T.bI2[:])
+        tt("Pm", "OH mu kcf", T.Pm[:], T.OH[:].indirect(T.mu[:]), T.kcf[:], A.mult)
+        tt("zc", "pZ cs", T.zc[:], T.pZ[:, 0:16], T.cs[:, 15:256:16], A.mult)
+        ts("a1", "zc", T.a1[:], T.zc[:], 0.0, None, A.is_lt)
+        ts("z4", "zc", T.z4[:], T.zc[:], -4.0, None, A.add)
+        if not last:
+            mm("pU", "a1 ON", T.pU[:, 0:16], T.ON[:], T.a1[:], True, True)
+        for j in range(16):
+            mm("pB", "Pm Q1f", T.pB[:, 0:16], T.Q1f[:, 15 - j:143 - j], T.Pm[:, j::16], j == 0, j == 15)
+        tt("m1", "sl1 a1", T.m1[:], T.sl1[:], T.a1[:], A.mult)
         ts("zy", "z4", T.zy[:], T.z4[:], 31, None, AND)
         ts("od", "z4", T.od[:], T.z4[:], 1, None, AND)
+        tt("m2", "m1 dm", T.m2[:], T.m1[:], T.dm[:], A.add)
         ts("b3", "zy", T.b3[:], T.zy[:], 5.0, None, A.is_lt)
+        if not last:
+            tt("um0", "pU Dg", T.um[:, 0:16], T.pU[:, 0:16], T.Dg[:], A.mult)
         tt("tn", "a1 b3", T.tn[:], T.a1[:], T.b3[:], A.add)
+        cp("SL", "m2", T.SL[:], T.m2[:])
+        if not last:
+            op("V", lambda: g.vector.tensor_reduce(T.um[:, 17:18], T.um[:, 0:17], AxisListType.X, A.add), "um2", "um0 um1")
         tt("mv0", "od tn", T.mv0[:], T.od[:], T.tn[:], A.is_gt)
+        if not last:
+            ts("uk", "um2", T.uk[:], T.um[:, 17:18], 1.0 / 256.0, -127.5 / 256.0, A.mult, A.add)
         tt("mv", "mv0 tn", T.mv[:, 0:15], T.mv0[:, 0:15], T.tn[:, 1:16], A.mult)
+        if not last:
+            ts("of%d" % ((t + 1) % 2), "uk um2", OF[(t + 1) % 2][:, 0:1], T.uk[:], -256.0, T.um[:, 17:18], A.mult, A.add)
         tt("tm", "mv tn", T.tm[:], T.tn[:], T.mv[:], A.add)
+        if not last:
+            tt(KK, "kcm cXm SL", T.K[:].indirect(T.SL[:]), T.kcm[:], T.cXm[:], A.add)
+        tt("db", "pB " + cfk, T.db[:], T.pB[:, 0:16], cf[:], A.subtract)
+        tt("dp", "pB " + cfk, T.dp[:, 0:15], cf[:, 0:15], T.pB[:, 1:16], A.subtract)
         tt("v1", "mv dp", T.v1[:, 0:15], T.mv[:, 0:15], T.dp[:, 0:15], A.mult)
         tt("u1", "tm db", T.u1[:], T.tm[:], T.db[:], A.mult)
         tt("nT", "u1 " + cfk, T.nT[:], T.u1[:], cf[:], A.add)
         tt("nT", "nT v1", T.nT[:, 1:16], T.nT[:, 1:16], T.v1[:, 0:15], A.add)
-        cp("Z", "nT offs", T.Z[:, 0:256].indirect(T.offs[:, 0:1]), T.nT[:])
+        cp("Z", "nT of%d" % (t % 2), T.Z[:, 0:256].indirect(OF[t % 2][:, 0:1]), T.nT[:])
         if not last:
-            ts("uk", "pU", T.uk[:], T.pU[:, 0:1], 1.0 / 256.0, -127.5 / 256.0, A.mult, A.add)
-            ts("offs", "uk pU", T.offs[:, 0:1], T.uk[:], -256.0, T.pU[:, 0:1], A.mult, A.add)
             draw(t + 1)
-            ts("iR", "pZ Rt", T.iR[:], T.pZ[:, 0:256], T.Rt[:, t:t + 1], None, A.is_lt)
-            tt("kd2", "iR kda kdb", T.kd2[:], T.iR[:], T.kd[:], A.mult)
-            tt("K Kd", "kcf kd2 SL", T.K[:].indirect(T.SL[:]), T.kcf[:], T.kd2[:], A.add)
 
     cp("Z2", "Z", T.Z[:, 256:512], T.Z[:, 0:256])
     dmas("Y", [(T.ZT[j::16, 0:256], T.Z[j::16, 16 * (-5 * j % 16):16 * (-5 * j % 16) + 256]) for j in range(16)], "dun", "ZT", "Z Z2")
-    tt("E Ed", "Ec iT SL", T.E[:].indirect(T.SL[:]), T.Ec[:], T.iT[:], A.add)
+    tt("E Ed", "Ec DBt SL", T.E[:].indirect(T.SL[:]), T.Ec[:], T.DBt[:, 0:256], A.add)
     for i in range(4):
         a, b = 768 * i, 768 * (i + 1)
-        act("LN%d" % i, "E", T.LN[:, a:b], T.E[:, a:b], F.Ln)
-        ts("YR%d" % i, "LN%d" % i, T.YR[:, a:b], T.LN[:, a:b], 1.0 / (6.0 * math.log(2.0)), 136.0, A.mult, A.add)
-        ts("YQ%d" % i, "YR%d" % i, T.YR2[:, a:b], T.YR[:, a:b], -128.0, None, A.add)
-        dmas("Y", [(T.yr[:, a:b], T.YR2[:, a:b])], "dy%d" % i, "", "YQ%d" % i)
+        act("LN%d IOTA" % i, "E", T.IOTA[:, a:b], T.E[:, a:b], F.Ln)
+        ts("YR%d Wt" % i, "LN%d" % i, T.Wt[:, a:b], T.IOTA[:, a:b], 1.0 / (6.0 * math.log(2.0)), 136.0, A.mult, A.add)
+        ts("YQ%d" % i, "YR%d" % i, T.recs[:, a:b], T.Wt[:, a:b], -128.0, None, A.add)
+        dmas("Y", [(T.yr[:, a:b], T.recs[:, a:b])], "dy%d" % i, "", "YQ%d" % i)
     cp("kc2", "ZT L2", T.kc2[:], T.ZT[:, 0:256].indirect(T.L2[:, 0:32]))
-    vtr("kTr", "kc2", T.kTr[:], T.kc2[:])
-    cp("ysb", "kTr LQ", T.ysb[:], T.kTr[:].indirect(T.LQ[:]))
-    dmas("Y", [(T.ys[:], T.ysb[:])], "dys", "", "ysb")
+    vtr("kTa kTb", "kc2", T.kTr[:], T.kc2[:])
+    cp("Pm", "kTa kTb LQ", T.Pm[:], T.kTr[:].indirect(T.LQ[:]))
+    dmas("Y", [(T.ys[:], T.Pm[:])], "dys", "", "Pm")
     for s in cnt:
         if clock["G"].get(s, 0) < cnt[s]:
             g.wait_ge(sem[s], cnt[s])

@@ -4,7 +4,9 @@ from concourse.mybir import ActivationFunctionType as F
 from concourse.mybir import AxisListType
 
 RO = 6
-EQ1 = 6
+WV = 4
+KS = 2
+EQ1 = 4
 NV = 32
 W = 3072
 WD = W + 256
@@ -26,22 +28,23 @@ _bufs("sbuf", WD, "bfloat16", "E")
 _bufs("sbuf", WD, "float32", "K")
 _bufs("sbuf", 4096, "bfloat16", "GE FE X")
 _bufs("sbuf", XB[16], "bfloat16", "EQT")
-_bufs("sbuf", 512, "float32", "Z ZT kc2 kTr D0")
+_bufs("sbuf", 512, "float32", "Z ZT kc2 kTr")
 _bufs("sbuf", 256, "int32", "slI rI rJ rB")
 _bufs("sbuf", 256, "uint16", "kcu fku kTu cbu")
-_bufs("sbuf", 256, "float32", "kcf kcm cXm S1s S1p sH Pm MJc cs MJ DB THR THJ riF tq")
+_bufs("sbuf", 256, "float32", "kcf kcm cXm Pm DB THR riF tq")
 _bufs("sbuf", 512, "bfloat16", "wc DT DBt")
-_bufs("sbuf", 256, "bfloat16", "Ec X1 X2 TIE")
+_bufs("sbuf", 128, "float32", "S1s t1 IDf NEG PX SW")
+_bufs("sbuf", 256, "bfloat16", "Ec X1 X2 TIE cb")
 _bufs("sbuf", 16, "int32", "bI bI2 z4 zy od")
-_bufs("sbuf", 16, "uint16", "mu SL cTs LM LQ LP")
-_bufs("sbuf", 16, "float32", "db dp cTf cTg sl1 m1 m2 zc b3 tn mv0 mv tm u1 v1 nT lane dm wcol Dg OH")
+_bufs("sbuf", 16, "uint16", "mu SL cTs LQ LP")
+_bufs("sbuf", 16, "float32", "cs cTf cTg m1 m2 zc b3 tn mv0 mv tm u1 v1 nT lane dm wcol Dg OH")
 _bufs("sbuf", 16, "bfloat16", "a1")
 _bufs("sbuf", 32, "uint16", "L1 L2 LZ")
 _bufs("sbuf", 32, "int32", "rH")
-_bufs("sbuf", 32, "float32", "um")
+_bufs("sbuf", 64, "float32", "t2")
+_bufs("sbuf", 32 * RO, "float32", "um")
 _bufs("sbuf", 128, "bfloat16", "BO ID ON")
-_bufs("sbuf", 128, "float32", "PX SW")
-_bufs("sbuf", 144, "bfloat16", "Q16 Q1 Q32")
+_bufs("sbuf", 144, "bfloat16", "Q16 Q1 Q32 QS")
 _bufs("sbuf", 144, "float32", "Q1f")
 _bufs("sbuf", 1, "int32", "pI xI gI hI oI uk")
 _bufs("sbuf", 1, "float32", "pF xF gF hF oF colA colB colC colD colE colF colG")
@@ -135,9 +138,6 @@ def rank_program(g, core, T, topo):
     def fill(w, ap, v):
         op("V", lambda: g.vector.memset(ap, v), w, "")
 
-    def scan(w, r, out, d1, o):
-        op("V", lambda: g.vector.tensor_tensor_scan(out, T.D0[:, 0:256], d1, 0.0, A.mult, o), w, r + " D0")
-
     def vtr(w, r, out, in_):
         op("V", lambda: g.vector.transpose(out, in_), w, r)
 
@@ -151,10 +151,6 @@ def rank_program(g, core, T, topo):
     for i in range(4):
         a, b = 768 * i, 768 * (i + 1)
         dmas("Y" if i < 2 else "S", [(T.kinI[:, a:b], T.kin[:, a:b])], "dk%d" % i, "kinI%d" % i, "")
-    for i in range(2):
-        a, b = 1536 * i, 1536 * (i + 1)
-        dmas("Y" if i else "S", [(T.recs[:, a:b], T.rec[:, a:b])], "dr%d" % i, "recs%d" % i, "")
-    dmas("S", [(T.Wt[:], T.wealth[:])], "dw", "Wt", "")
 
     op("G", lambda: g.iota(T.pI[:], [[0, 1]], 0, 1), "pI", "")
     op("G", lambda: g.iota(T.rI[:], [[1, 256]], 0, 0), "rI", "")
@@ -175,6 +171,10 @@ def rank_program(g, core, T, topo):
     vtr("kTa kTb", "kc2", T.kTr[:], T.kc2[:])
     cp("ZT", "kTa kTb LZ", T.ZT[:], T.kTr[:].indirect(T.LZ[:, 0:32]))
     dmas("Y", [(T.Z[j::16, 0:256], T.ZT[j::16, 16 * (5 * j % 16):16 * (5 * j % 16) + 256]) for j in range(16)], "dsh", "Z", "ZT")
+    for i in range(2):
+        a, b = 1536 * i, 1536 * (i + 1)
+        dmas("Y", [(T.recs[:, a:b], T.rec[:, a:b])], "dr%d" % i, "recs%d" % i, "")
+    dmas("Y", [(T.Wt[:], T.wealth[:])], "dw", "Wt", "")
     fill("Ed", T.E[:, W:WD], 0.0)
     fill("Kd", T.K[:, W:WD], 0.0)
     ts("rB", "rI", T.rB[:], T.rI[:], 4, None, SH)
@@ -182,63 +182,60 @@ def rank_program(g, core, T, topo):
     cp("pF", "pI", T.pF[:], T.pI[:])
     cp("gF", "gI", T.gF[:], T.gI[:])
     ts("ID", "rI pF", T.ID[:], T.rI[:, 0:128], T.pF[:], None, A.is_equal)
-    for i in range(2):
-        a, b = 1536 * i, 1536 * (i + 1)
-        act("E", "recs%d eb" % i, T.E[:, a:b], T.recs[:, a:b], F.Exp, bias=T.eb[:, 2:3], scale=6.0 * math.log(2.0))
+    ts("colG", "hF pF", T.colG[:], T.hF[:], -2.0, T.pF[:], A.mult, A.add)
+    ts("colG", "colG", T.colG[:], T.colG[:], 16.0, None, A.add)
+    ts("SW", "rI colG", T.SW[:], T.rI[:, 0:128], T.colG[:], None, A.is_equal)
+    ts("oI", "pI", T.oI[:], T.pI[:], 1, None, AND)
+    cp("oF", "oI", T.oF[:], T.oI[:])
+    ts("gI", "hI", T.gI[:], T.hI[:], 4, None, SH)
+    tt("colF", "oF gI", T.colF[:], T.oF[:], T.gI[:], A.not_equal)
+    ts("xI", "xI", T.xI[:], T.xI[:], 1, None, SH)
+    ts("colE", "xI hF", T.colE[:], T.xI[:], 32.0, T.hF[:], A.mult, A.add)
+    ts("colF", "colF colE", T.colF[:], T.colF[:], 256.0, T.colE[:], A.mult, A.add)
+    ts("LP", "rI colF", T.LP[:], T.rI[:, 0:16], T.colF[:], None, A.add)
+    LB = math.log(BASE)
+    ts("colC", "xF", T.colC[:], T.xF[:], 16.0, None, A.mult)
+    ts("colD", "gF", T.colD[:], T.gF[:], 16.0, 15.0, A.mult, A.add)
+    tt("colB", "xF hF", T.colB[:], T.xF[:], T.hF[:], A.add)
+    ts("lane", "rI xF", T.lane[:], T.rI[:, 0:16], 16.0, T.xF[:], A.mult, A.add)
+    fill("eb0", T.eb[:, 0:1], 71.0)
+    fill("eb1", T.eb[:, 1:2], 71.0 + math.log(2.53))
+    cp("riF", "rI", T.riF[:], T.rI[:])
+    act("wcol", "lane eb0", T.wcol[:], T.lane[:], F.Exp, bias=T.eb[:, 0:1], scale=-LB)
+    act("THR", "riF eb1", T.THR[:], T.riF[:], F.Exp, bias=T.eb[:, 1:2], scale=-LB)
+    ts("Q16", "rI colD", T.Q16[:], T.rI[:, 0:144], T.colD[:], 16.0, A.is_equal, A.mult)
+    ts("Q1", "rI colD", T.Q1[:], T.rI[:, 0:144], T.colD[:], None, A.is_equal)
+    ts("Q32", "rI colD", T.Q32[:], T.rI[:, 0:144], T.colD[:], 32.0, A.is_equal, A.mult)
+    ts("QS", "rI colD", T.QS[:], T.rI[:, 0:144], T.colD[:], 1.0 / 16.0, A.is_equal, A.mult)
+    ts("Q1f", "rI colD", T.Q1f[:], T.rI[:, 0:144], T.colD[:], None, A.is_equal)
+    ts("BO", "rB gF", T.BO[:], T.rB[:, 0:128], T.gF[:], None, A.is_equal)
+    ts("TIE", "rB", T.TIE[:], T.rB[:], -1.0, 15.0, A.mult, A.add)
+    ts("DB", "rB xF", T.DB[:], T.rB[:], T.xF[:], None, A.is_equal)
     for i in range(4):
         a, b = 768 * i, 768 * (i + 1)
         cp("K%d" % i, "kinI%d" % i, T.K[:, a:b], T.kinI[:, a:b])
     KK = "K0 K1 K2 K3 Kd"
-    LB = math.log(BASE)
 
-    def swap_constants():
-        ts("colG", "hF pF", T.colG[:], T.hF[:], -2.0, T.pF[:], A.mult, A.add)
-        ts("colG", "colG", T.colG[:], T.colG[:], 16.0, None, A.add)
-        ts("SW", "rI colG", T.SW[:], T.rI[:, 0:128], T.colG[:], None, A.is_equal)
-        ts("oI", "pI", T.oI[:], T.pI[:], 1, None, AND)
-        cp("oF", "oI", T.oF[:], T.oI[:])
-        ts("gI", "hI", T.gI[:], T.hI[:], 4, None, SH)
-        tt("colF", "oF gI", T.colF[:], T.oF[:], T.gI[:], A.not_equal)
-        ts("xI", "xI", T.xI[:], T.xI[:], 1, None, SH)
-        ts("colE", "xI hF", T.colE[:], T.xI[:], 32.0, T.hF[:], A.mult, A.add)
-        ts("colF", "colF colE", T.colF[:], T.colF[:], 256.0, T.colE[:], A.mult, A.add)
-        ts("LP", "rI colF", T.LP[:], T.rI[:, 0:16], T.colF[:], None, A.add)
-
-    def late_constants():
-        ts("colC", "xF", T.colC[:], T.xF[:], 16.0, None, A.mult)
-        ts("colD", "gF", T.colD[:], T.gF[:], 16.0, 15.0, A.mult, A.add)
-        tt("colB", "xF hF", T.colB[:], T.xF[:], T.hF[:], A.add)
-        ts("lane", "rI xF", T.lane[:], T.rI[:, 0:16], 16.0, T.xF[:], A.mult, A.add)
-        fill("eb0", T.eb[:, 0:1], 71.0)
-        fill("eb1", T.eb[:, 1:2], 71.0 + math.log(2.53))
-        cp("riF", "rI", T.riF[:], T.rI[:])
-        act("wcol", "lane eb0", T.wcol[:], T.lane[:], F.Exp, bias=T.eb[:, 0:1], scale=-LB)
-        act("THR", "riF eb1", T.THR[:], T.riF[:], F.Exp, bias=T.eb[:, 1:2], scale=-LB)
-        ts("Q16", "rI colD", T.Q16[:], T.rI[:, 0:144], T.colD[:], 16.0, A.is_equal, A.mult)
-        ts("Q1", "rI colD", T.Q1[:], T.rI[:, 0:144], T.colD[:], None, A.is_equal)
-        ts("Q32", "rI colD", T.Q32[:], T.rI[:, 0:144], T.colD[:], 32.0, A.is_equal, A.mult)
-        ts("Q1f", "rI colD", T.Q1f[:], T.rI[:, 0:144], T.colD[:], None, A.is_equal)
-        ts("BO", "rB gF", T.BO[:], T.rB[:, 0:128], T.gF[:], None, A.is_equal)
-        ts("TIE", "rB", T.TIE[:], T.rB[:], -1.0, 15.0, A.mult, A.add)
-        ts("LM", "rI colC", T.LM[:], T.rI[:, 0:16], T.colC[:], None, A.add)
-        ts("D0", "rJ", T.D0[:, 0:256], T.rJ[:], 0.0, None, A.is_gt)
-        ts("MJ", "rJ xF", T.MJ[:], T.rJ[:], T.xF[:], None, A.is_equal)
-        ts("DB", "rB xF", T.DB[:], T.rB[:], T.xF[:], None, A.is_equal)
+    def records():
+        for i in range(2):
+            a, b = 1536 * i, 1536 * (i + 1)
+            act("E", "recs%d eb" % i, T.E[:, a:b], T.recs[:, a:b], F.Exp, bias=T.eb[:, 2:3], scale=6.0 * math.log(2.0))
 
     def later_constants():
         ts("dm", "lane", T.dm[:], T.lane[:], float(W), None, A.add)
-        tt("THJ", "THR MJ", T.THJ[:], T.THR[:], T.MJ[:], A.mult)
-        ts("tq", "MJ", T.tq[:], T.MJ[:], -1.0, None, A.add)
-        tt("THJ", "THJ tq", T.THJ[:], T.THJ[:], T.tq[:], A.add)
-        ts("riF", "DB THR", T.riF[:], T.DB[:], -1e20, 1e20, A.mult, A.add)
+        ts("IDf", "rI pF", T.IDf[:], T.rI[:, 0:128], T.pF[:], None, A.is_equal)
+        ts("NEG", "rI pF", T.NEG[:], T.rI[:, 0:128], T.pF[:], -1.0, A.is_equal, A.mult)
+        for t in range(1, RO):
+            ts("um1", "colC", T.um[:, 32 * t + 16:32 * t + 17], T.colC[:], 1.0 / 16.0, 16.0 * t, A.mult, A.add)
+        ts("riF", "DB", T.riF[:], T.DB[:], -1e20, 1e20, A.mult, A.add)
         ts("tq", "DB", T.tq[:], T.DB[:], 0.9 * 64.0 ** -3, None, A.mult)
-        tt("DT0", "tq riF", T.DT[:, 0:256], T.tq[:], T.riF[:], A.max)
         ts("colE", "xF", T.colE[:], T.xF[:], -1.0, 15.0, A.mult, A.add)
-        ts("OH", "rI colE", T.OH[:], T.rI[:, 0:16], T.colE[:], None, A.is_equal)
         ts("colF", "oF pF", T.colF[:], T.oF[:], -2.0, T.pF[:], A.mult, A.add)
+        tt("DT0", "tq riF", T.DT[:, 0:256], T.tq[:], T.riF[:], A.max)
+        ts("OH", "rI colE", T.OH[:], T.rI[:, 0:16], T.colE[:], None, A.is_equal)
         ts("colF", "colF", T.colF[:], T.colF[:], 1.0, None, A.add)
-        ts("PX", "rI colF", T.PX[:], T.rI[:, 0:128], T.colF[:], None, A.is_equal)
         ts("Dg", "rI xF", T.Dg[:], T.rI[:, 0:16], T.xF[:], 16.0, A.is_equal, A.mult)
+        ts("PX", "rI colF", T.PX[:], T.rI[:, 0:128], T.colF[:], None, A.is_equal)
         ts("Ne", "rI xF", T.Ne[:, 0:RO], T.rI[:, 0:RO], T.xF[:], None, A.is_equal)
         ts("Nn", "rI xF", T.Nn[:, 0:RO], T.rI[:, 0:RO], T.xF[:], None, A.not_equal)
         ts("LQ", "rI colB", T.LQ[:], T.rI[:, 0:16], 32.0, T.colB[:], A.mult, A.add)
@@ -246,13 +243,13 @@ def rank_program(g, core, T, topo):
         fill("ON", T.ON[:], 1.0)
         fill("mv", T.mv[:], 0.0)
 
-    def remote(dst, out, in_, rs, r, w):
+    def remote(dst, out, in_, rs, r):
         eng = topo.engines(core, dst)[::2]
         m = 0
         for e in eng:
             m |= 1 << e
         rid, pid, _ = topo.addr(dst)
-        dep("G", r.split(), w.split())
+        dep("G", r.split(), [])
         g.remote_dma(out, in_, sem[rs], sem.ls, pid, rid, m)
         cnt["ls"] = cnt.get("ls", 0) + len(eng)
         return len(eng)
@@ -261,10 +258,6 @@ def rank_program(g, core, T, topo):
 
     def draw(t):
         cp("cTu%d" % t, "Z of%d" % (t % 2), T.cTu[:, 16 * t:16 * t + 16], T.Z[:, 0:256].indirect(OF[t % 2][:, 0:1]))
-
-    def draw_more(t):
-        f = ("cTf", T.cTf) if t % 2 == 0 else ("cTg", T.cTg)
-        cp(f[0], "cTu%d" % t, f[1][:], T.cTu[:, 16 * t:16 * t + 16])
 
     ident = T.ID[:]
     Ew, Kw, Ww, Iw = T.E[:, 0:W], T.K[:, 0:W], T.Wt[:], T.IOTA[:]
@@ -288,27 +281,32 @@ def rank_program(g, core, T, topo):
         cuk = "cTu%d" % t
         cfk, cf = ("cTf", T.cTf) if t % 2 == 0 else ("cTg", T.cTg)
         last = t == RO - 1
+        u = 32 * (t + 1)
         dtk, dt_ = "DT%d" % (t % 2), T.DT[:, 256 * (t % 2):256 * (t % 2) + 256]
-        ne = remote(asked, T.ql[:, 16 * t:16 * t + 16], cu, "qa%d" % t, cuk, "")
+        ne = remote(asked, T.ql[:, 16 * t:16 * t + 16], cu, "qa%d" % t, cuk)
         lastw["ql%d" % t] = ("qa%d" % t, ne)
         lastw["rl%d" % t] = ("ra%d" % t, ne)
-        cp("kcu", KK + " " + cuk, T.kcu[:], Kw.indirect(cu))
+        act(cfk, "Z of%d" % (t % 2), cf[:], T.Z[:, 0:256].indirect(OF[t % 2][:, 0:1]))
         act("kcf", KK + " " + cuk, T.kcf[:], Kw.indirect(cu))
-        if t > 0:
+
+        def own_wealth():
+            act("wc", "Wt " + cuk, T.wc[:, 0:256], Ww.indirect(cu))
+            act("wcb", "Wt " + cuk, T.wc[:, 256:512], Ww.indirect(cu))
+        if t == 0:
+            records()
+        else:
+            own_wealth()
             tt("E Ed", "Ec DBt SL", T.E[:].indirect(T.SL[:]), T.Ec[:], T.DBt[:, 0:256], A.add)
-        act("wc", "Wt " + cuk, T.wc[:, 0:256], Ww.indirect(cu))
-        act("wcb", "Wt " + cuk, T.wc[:, 256:512], Ww.indirect(cu))
+        cp("kcu", "kcf", T.kcu[:], T.kcf[:])
         act("Ec", "E " + cuk, T.Ec[:], Ew.indirect(cu))
         vtr("kTa", "kcf", T.kTr[:, 0:256], T.kcf[:])
-        if t == 0:
-            swap_constants()
         mm("pX", "kTa SW", T.pX[:, 0:256], T.SW[:], T.kTr[:, 0:256], True, True)
         act("kTb", "pX", T.kTr[:, 256:512], T.pX[:, 0:256])
-        draw_more(t)
         cp("cbu", "IOTA " + cuk, T.cbu[:], Iw.indirect(cu))
-        if t == 0:
-            late_constants()
         gather_e("S", T.GE, "GE0", T.kcu, "kcu", 0, 64)
+        if t == 0:
+            own_wealth()
+            later_constants()
         mm("pES", "Ec ID", T.pES[:, 0:256], ident, T.Ec[:], True, False)
         sum_e(T.pES, "pES", T.GE, "GE0", 0, 64, False, False)
 
@@ -322,50 +320,64 @@ def rank_program(g, core, T, topo):
 
         def wealth(m):
             tt("X%d" % m, "Wt kTu wc wcb", T.X[:, 512 * m:512 * m + 512], Ww.indirect(T.kTu[:, 32 * m:32 * m + 32]), T.wc[:], A.max)
+
+        def score(h):
+            mm("pS1", "TIE ID", T.pS1[:, 128 * h:128 * h + 128], ident, T.TIE[:, 128 * h:128 * h + 128], True, False)
+            xs = " ".join("X%d" % m for m in range(4 * h, 4 * h + 4))
+            for j in range(16):
+                mm("pS1", xs + " Q16", T.pS1[:, 128 * h:128 * h + 128], T.Q16[:, 15 - j:143 - j], T.X[:, 2048 * h + j:2048 * h + 2048:16], False, j == 15)
         for b in range(EQ1):
             equal(b)
         cp("kTu", "kTa kTb LP", T.kTu[:], T.kTr[:].indirect(T.LP[:]))
         cp("fku", KK + " ql%d" % t, T.fku[:], Kw.indirect(T.ql[:, 16 * t:16 * t + 16]))
-        for m in range(8):
+        for m in range(WV):
+            wealth(m)
+        gather_e("V", T.FE, "FE3", T.fku, "fku", 192, 64)
+        for m in range(WV, 8):
             wealth(m)
         for b in range(EQ1):
             equal_sum(b)
-        for k in range(4):
+        for k in range(3):
             gather_e("S", T.FE, "FE%d" % k, T.fku, "fku", 64 * k, 64)
-            sum_e(T.pFS, "pFS", T.FE, "FE%d" % k, 64 * k, 64, True, True)
+        for k in range(4):
+            if k == KS:
+                score(0)
+            p = (0, 1, 3, 2)[k]
+            sum_e(T.pFS, "pFS", T.FE, "FE%d" % p, 64 * p, 64, True, True)
         gather_e("S", T.GE, "GE1", T.kcu, "kcu", 64, 32)
-        mm("pS1", "TIE ID", T.pS1[:, 0:256], ident, T.TIE[:], True, False)
-        xs = " ".join("X%d" % m for m in range(8))
-        for j in range(16):
-            mm("pS1", xs + " Q16", T.pS1[:, 0:256], T.Q16[:, 15 - j:143 - j], T.X[:, j::16], False, j == 15)
         fs = T.fs[:, 256 * t:256 * t + 256]
         act("fs%d" % t, "pFS", fs, T.pFS[:, 0:256])
-        remote(asker, T.rl[:, 256 * t:256 * t + 256], fs, "ra%d" % t, "fs%d" % t, "")
+        remote(asker, T.rl[:, 256 * t:256 * t + 256], fs, "ra%d" % t, "fs%d" % t)
+        score(1)
         gather_e("S", T.GE, "GE1b", T.kcu, "kcu", 96, 32)
         gather_e("S", T.GE, "GE2", T.kcu, "kcu", 128, 64)
-        act("S1s", "pS1", T.S1s[:], T.pS1[:, 0:256])
+        act("S1s", "pS1", T.S1s[:], T.pS1[:, 128:256])
         if NV < 64:
             gather_e("S", T.GE, "GE3", T.kcu, "kcu", 192, 64 - NV)
-        if t == 0:
-            later_constants()
         for b in range(EQ1, 16):
             equal(b)
             equal_sum(b)
         sum_e(T.pES, "pES", T.GE, "GE1 GE1b", 64, 64, False, False)
-        tt("sl1", "dm " + cfk, T.sl1[:], cf[:], T.dm[:], A.subtract)
         if not last:
             mm("pX", "PX " + cfk, T.pX[:, 0:16], T.PX[:], cf[:], True, True)
-        gather_e("V", T.GE, "GE4", T.kcu, "kcu", 256 - NV, NV)
-        tt("MJc", "pEQ THJ", T.MJc[:], T.pEQ[:, 0:256], T.THJ[:], A.is_lt)
+        mm("pX", "IDf " + cfk, T.pX[:, 16:32], T.IDf[:], cf[:], True, False)
+        mm("pX", "NEG dm", T.pX[:, 16:32], T.NEG[:], T.dm[:], False, True)
+        if NV:
+            gather_e("V", T.GE, "GE4", T.kcu, "kcu", 256 - NV, NV)
+        tt("cb", "pEQ THR", T.cb[:], T.pEQ[:, 0:256], T.THR[:], A.is_lt)
         if not last:
             cp("cTs", "pX", T.cTs[:], T.pX[:, 0:16])
-            ts("um1", "rI colC", T.um[:, 16:17], T.colC[:], 1.0 / 16.0, 16.0 * (t + 1), A.mult, A.add)
-        scan("cs", "MJc", T.cs[:], T.MJc[:], A.add)
         sum_e(T.pES, "pES", T.GE, "GE2", 128, 64, False, False)
+        tt("t1", "pS1 S1s", T.t1[:], T.pS1[:, 0:128], T.S1s[:], A.max)
         sum_e(T.pES, "pES", T.GE, "GE3 GE4", 192, 64, False, False)
         mm("pES", "rl%d ID" % t, T.pES[:, 0:256], ident, T.rl[:, 256 * t:256 * t + 256], False, True)
-        cp("S1p", "S1s LM", T.S1p[:], T.S1s[:].indirect(T.LM[:]))
-        scan("sH", "S1p", T.sH[:], T.S1p[:], A.max)
+        for j in range(16):
+            mm("pX", "cb QS", T.pX[:, 32:48], T.QS[:, 15 - j:143 - j], T.cb[:, j::16], j == 0, j == 15)
+        act("cs", "pX", T.cs[:], T.pX[:, 32:48])
+        tt("t2", "t1", T.t2[:], T.t1[:, 0:64], T.t1[:, 64:128], A.max)
+        mm("pB", "IDf " + cfk, T.pB[:, 32:47], T.IDf[:], cf[:, 0:15], True, False)
+        mm("pB", "NEG " + cfk, T.pB[:, 32:47], T.NEG[:], cf[:, 1:16], False, True)
+        tt("t3", "t2", T.t1[:, 0:32], T.t2[:, 0:32], T.t2[:, 32:64], A.max)
         if not last:
             act("kcm", "kcf Nn", T.kcm[:], T.kcf[:], F.Copy, scale=T.Nn[:, t:t + 1])
             act("cXm", "IOTA Ne cTs", T.cXm[:], Iw.indirect(T.cTs[:]), F.Copy, scale=T.Ne[:, t:t + 1])
@@ -379,41 +391,43 @@ def rank_program(g, core, T, topo):
         tt("X2", "pES " + dtk, T.X2[:], T.pES[:, 0:256], dt_, A.is_ge)
         for j in range(16):
             mm("pZ", "X2 Q32", T.pZ[:, 0:16], T.Q32[:, 15 - j:143 - j], T.X2[:, j::16], False, j == 15)
-        cp("bI", "sH", T.bI[:], T.sH[:, 15:256:16])
+        tt("bI", "t3", T.bI[:], T.t1[:, 0:16], T.t1[:, 16:32], A.max)
         ts("bI2", "bI", T.bI2[:], T.bI[:], 15, None, AND)
         cp("mu", "bI2", T.mu[:], T.bI2[:])
         tt("Pm", "OH mu kcf", T.Pm[:], T.OH[:].indirect(T.mu[:]), T.kcf[:], A.mult)
-        tt("zc", "pZ cs", T.zc[:], T.pZ[:, 0:16], T.cs[:, 15:256:16], A.mult)
+        tt("zc", "pZ cs", T.zc[:], T.pZ[:, 0:16], T.cs[:], A.mult)
         ts("a1", "zc", T.a1[:], T.zc[:], 0.0, None, A.is_lt)
         ts("z4", "zc", T.z4[:], T.zc[:], -4.0, None, A.add)
         if not last:
             mm("pU", "a1 ON", T.pU[:, 0:16], T.ON[:], T.a1[:], True, True)
+        mm("pB", "NEG " + cfk, T.pB[:, 0:16], T.NEG[:], cf[:], True, False)
         for j in range(16):
-            mm("pB", "Pm Q1f", T.pB[:, 0:16], T.Q1f[:, 15 - j:143 - j], T.Pm[:, j::16], j == 0, j == 15)
-        tt("m1", "sl1 a1", T.m1[:], T.sl1[:], T.a1[:], A.mult)
+            mm("pB", "Pm Q1f", T.pB[:, 0:16], T.Q1f[:, 15 - j:143 - j], T.Pm[:, j::16], False, j == 15)
+        tt("m1", "pX a1", T.m1[:], T.pX[:, 16:32], T.a1[:], A.mult)
         ts("zy", "z4", T.zy[:], T.z4[:], 31, None, AND)
         ts("od", "z4", T.od[:], T.z4[:], 1, None, AND)
         tt("m2", "m1 dm", T.m2[:], T.m1[:], T.dm[:], A.add)
         ts("b3", "zy", T.b3[:], T.zy[:], 5.0, None, A.is_lt)
         if not last:
-            tt("um0", "pU Dg", T.um[:, 0:16], T.pU[:, 0:16], T.Dg[:], A.mult)
+            tt("um0", "pU Dg", T.um[:, u:u + 16], T.pU[:, 0:16], T.Dg[:], A.mult)
         tt("tn", "a1 b3", T.tn[:], T.a1[:], T.b3[:], A.add)
         cp("SL", "m2", T.SL[:], T.m2[:])
         if not last:
-            op("V", lambda: g.vector.tensor_reduce(T.um[:, 17:18], T.um[:, 0:17], AxisListType.X, A.add), "um2", "um0 um1")
+            op("V", lambda: g.vector.tensor_reduce(T.um[:, u + 17:u + 18], T.um[:, u:u + 17], AxisListType.X, A.add), "um2", "um0 um1")
         tt("mv0", "od tn", T.mv0[:], T.od[:], T.tn[:], A.is_gt)
         if not last:
-            ts("uk", "um2", T.uk[:], T.um[:, 17:18], 1.0 / 256.0, -127.5 / 256.0, A.mult, A.add)
+            ts("uk", "um2", T.uk[:], T.um[:, u + 17:u + 18], 1.0 / 256.0, -127.5 / 256.0, A.mult, A.add)
         tt("mv", "mv0 tn", T.mv[:, 0:15], T.mv0[:, 0:15], T.tn[:, 1:16], A.mult)
         if not last:
-            ts("of%d" % ((t + 1) % 2), "uk um2", OF[(t + 1) % 2][:, 0:1], T.uk[:], -256.0, T.um[:, 17:18], A.mult, A.add)
+            ts("of%d" % ((t + 1) % 2), "uk um2", OF[(t + 1) % 2][:, 0:1], T.uk[:], -256.0, T.um[:, u + 17:u + 18], A.mult, A.add)
         tt("tm", "mv tn", T.tm[:], T.tn[:], T.mv[:], A.add)
         if not last:
             tt(KK, "kcm cXm SL", T.K[:].indirect(T.SL[:]), T.kcm[:], T.cXm[:], A.add)
-        tt("db", "pB " + cfk, T.db[:], T.pB[:, 0:16], cf[:], A.subtract)
-        tt("dp", "pB " + cfk, T.dp[:, 0:15], cf[:, 0:15], T.pB[:, 1:16], A.subtract)
-        tt("v1", "mv dp", T.v1[:, 0:15], T.mv[:, 0:15], T.dp[:, 0:15], A.mult)
-        tt("u1", "tm db", T.u1[:], T.tm[:], T.db[:], A.mult)
+        else:
+            tt("E Ed", "Ec DBt SL", T.E[:].indirect(T.SL[:]), T.Ec[:], T.DBt[:, 0:256], A.add)
+        tt("tm", "tm mv", T.tm[:, 1:16], T.tm[:, 1:16], T.mv[:, 0:15], A.subtract)
+        tt("v1", "mv pB", T.v1[:, 0:15], T.mv[:, 0:15], T.pB[:, 32:47], A.mult)
+        tt("u1", "tm pB", T.u1[:], T.tm[:], T.pB[:, 0:16], A.mult)
         tt("nT", "u1 " + cfk, T.nT[:], T.u1[:], cf[:], A.add)
         tt("nT", "nT v1", T.nT[:, 1:16], T.nT[:, 1:16], T.v1[:, 0:15], A.add)
         cp("Z", "nT of%d" % (t % 2), T.Z[:, 0:256].indirect(OF[t % 2][:, 0:1]), T.nT[:])
@@ -422,11 +436,13 @@ def rank_program(g, core, T, topo):
 
     cp("Z2", "Z", T.Z[:, 256:512], T.Z[:, 0:256])
     dmas("Y", [(T.ZT[j::16, 0:256], T.Z[j::16, 16 * (-5 * j % 16):16 * (-5 * j % 16) + 256]) for j in range(16)], "dun", "ZT", "Z Z2")
-    tt("E Ed", "Ec DBt SL", T.E[:].indirect(T.SL[:]), T.Ec[:], T.DBt[:, 0:256], A.add)
     for i in range(4):
         a, b = 768 * i, 768 * (i + 1)
         act("LN%d IOTA" % i, "E", T.IOTA[:, a:b], T.E[:, a:b], F.Ln)
-        ts("YR%d Wt" % i, "LN%d" % i, T.Wt[:, a:b], T.IOTA[:, a:b], 1.0 / (6.0 * math.log(2.0)), 136.0, A.mult, A.add)
+        if i == 3:
+            act("YR3", "LN3", T.Wt[:, a:b], T.IOTA[:, a:b], F.Identity, bias=136.0, scale=1.0 / (6.0 * math.log(2.0)))
+        else:
+            ts("YR%d" % i + ("" if i else " Wt"), "LN%d" % i, T.Wt[:, a:b], T.IOTA[:, a:b], 1.0 / (6.0 * math.log(2.0)), 136.0, A.mult, A.add)
         ts("YQ%d" % i, "YR%d" % i, T.recs[:, a:b], T.Wt[:, a:b], -128.0, None, A.add)
         dmas("Y", [(T.yr[:, a:b], T.recs[:, a:b])], "dy%d" % i, "", "YQ%d" % i)
     cp("kc2", "ZT L2", T.kc2[:], T.ZT[:, 0:256].indirect(T.L2[:, 0:32]))

import math
from concourse.mybir import AluOpType as A
from concourse.mybir import ActivationFunctionType as F
from concourse.mybir import AxisListType

RO = 6
WV = 4
KS = 2
EQ1 = 4
NV = 32
W = 3072
WD = W + 256
BASE = 1.75
XB = [256 * b - 8 * b * (b - 1) for b in range(17)]

SCRATCH = {}


def _bufs(where, n, dtype, names):
    for k in names.split():
        SCRATCH[k] = (where, [128, n], dtype)


_bufs("sbuf", W, "bfloat16", "recs Wt")
_bufs("sbuf", W, "int32", "kinI")
_bufs("sbuf", W, "float32", "IOTA")
_bufs("sbuf", WD, "bfloat16", "E")
_bufs("sbuf", WD, "float32", "K")
_bufs("sbuf", 4096, "bfloat16", "GE FE X")
_bufs("sbuf", XB[16], "bfloat16", "EQT")
_bufs("sbuf", 512, "float32", "Z ZT kc2 kTr")
_bufs("sbuf", 256, "int32", "slI rI rJ rB")
_bufs("sbuf", 256, "uint16", "kcu fku kTu cbu")
_bufs("sbuf", 256, "float32", "kcf kcm cXm Pm DB THR riF tq")
_bufs("sbuf", 512, "bfloat16", "wc DT DBt")
_bufs("sbuf", 128, "float32", "S1s t1 IDf NEG PX SW")
_bufs("sbuf", 256, "bfloat16", "Ec X1 X2 TIE cb")
_bufs("sbuf", 16, "int32", "bI bI2 z4 zy od")
_bufs("sbuf", 16, "uint16", "mu SL cTs LQ LP")
_bufs("sbuf", 16, "float32", "cs cTf cTg m1 m2 zc b3 tn mv0 mv tm u1 v1 nT lane dm wcol Dg OH")
_bufs("sbuf", 16, "bfloat16", "a1")
_bufs("sbuf", 32, "uint16", "L1 L2 LZ")
_bufs("sbuf", 32, "int32", "rH")
_bufs("sbuf", 64, "float32", "t2")
_bufs("sbuf", 32 * RO, "float32", "um")
_bufs("sbuf", 128, "bfloat16", "BO ID ON")
_bufs("sbuf", 144, "bfloat16", "Q16 Q1 Q32 QS")
_bufs("sbuf", 144, "float32", "Q1f")
_bufs("sbuf", 1, "int32", "pI xI gI hI oI uk")
_bufs("sbuf", 1, "float32", "pF xF gF hF oF colA colB colC colD colE colF colG")
_bufs("sbuf", 8, "float32", "eb Ne Nn")
_bufs("sbuf", 2, "uint16", "of0 of1")
_bufs("psum", 512, "float32", "pES pFS pEQ pS1 pZ pU pB pX")
_bufs("sbuf", 16 * RO, "uint16", "cTu ql")
_bufs("sbuf", 256 * RO, "bfloat16", "fs rl")
SEMAPHORES = ["sv", "ss", "sp", "sg", "ls", "dsl", "dsh", "dun", "dys", "dw"] + ["dk%d" % i for i in range(4)] + ["dr%d" % i for i in range(2)] + ["dy%d" % i for i in range(4)] \
    + ["qa%d" % t for t in range(RO)] + ["ra%d" % t for t in range(RO)]


def rank_program(g, core, T, topo):
    rank = T.rank_of(core)
    if rank is None:
        return
    sem = T.sem
    ENG = {"V": g.vector, "S": g.scalar, "P": g.tensor, "G": g, "Y": g.sync}
    SEM = {"V": "sv", "S": "ss", "P": "sp", "G": "sg"}
    cnt = {}
    clock = {"V": {}, "S": {}, "P": {}, "G": {}, "Y": {}}
    snap = {}
    lastw = {}
    lastr = {}

    def dep(q, r, w):
        need = {}

        def add(tok, war):
            s, n = tok
            if war and q == "P" and s == "sp":
                return
            if need.get(s, 0) < n:
                need[s] = n
        for k in r:
            if k in lastw:
                add(lastw[k], False)
        for k in w:
            if k in lastw:
                add(lastw[k], True)
            for s, n in lastr.get(k, {}).items():
                add((s, n), True)
        ck = clock[q]
        for s in sorted(need, key=lambda s: -len(snap.get((s, need[s]), {}))):
            n = need[s]
            if ck.get(s, 0) < n:
                ENG[q].wait_ge(sem[s], n)
                ck[s] = n
                for s2, n2 in snap.get((s, n), {}).items():
                    if ck.get(s2, 0) < n2:
                        ck[s2] = n2

    def mark(q, tok, r, w):
        snap[tok] = dict(clock[q])
        for k in w:
            lastw[k] = tok
            lastr[k] = {}
        for k in r:
            d = lastr.setdefault(k, {})
            if d.get(tok[0], 0) < tok[1]:
                d[tok[0]] = tok[1]

    def op(q, fn, w, r):
        w, r = w.split(), r.split()
        dep(q, r, w)
        s = SEM[q]
        fn().then_inc(sem[s], 1)
        cnt[s] = cnt.get(s, 0) + 1
        mark(q, (s, cnt[s]), r, w)

    def dmas(q, pairs, s, w, r):
        w, r = w.split(), r.split()
        dep(q, r, w)
        for o, i in pairs:
            ENG[q].dma_start(o, i).then_inc(sem[s], 16)
            cnt[s] = cnt.get(s, 0) + 16
        mark(q, (s, cnt[s]), r, w)

    def ts(w, r, out, in0, s1, s2, op0, op1=None):
        if op1 is None:
            op("V", lambda: g.vector.tensor_scalar(out, in0, s1, None, op0), w, r)
        else:
            op("V", lambda: g.vector.tensor_scalar(out, in0, s1, s2, op0, op1), w, r)

    def tt(w, r, out, a, b, o):
        op("V", lambda: g.vector.tensor_tensor(out, a, b, o), w, r)

    def cp(w, r, out, in_):
        op("V", lambda: g.vector.tensor_copy(out, in_), w, r)

    def fill(w, ap, v):
        op("V", lambda: g.vector.memset(ap, v), w, "")

    def vtr(w, r, out, in_):
        op("V", lambda: g.vector.transpose(out, in_), w, r)

    def act(w, r, out, in_, f=F.Copy, bias=0.0, scale=1.0):
        op("S", lambda: g.scalar.activation(out, in_, f, bias=bias, scale=scale), w, r)

    def mm(w, r, out, l, x, st, sp):
        op("P", lambda: g.tensor.matmul(out, l, x, st, sp), w, r)

    dmas("Y", [(T.slI[:], T.slips[:])], "dsl", "slI", "")
    for i in range(4):
        a, b = 768 * i, 768 * (i + 1)
        dmas("Y" if i < 2 else "S", [(T.kinI[:, a:b], T.kin[:, a:b])], "dk%d" % i, "kinI%d" % i, "")

    op("G", lambda: g.iota(T.pI[:], [[0, 1]], 0, 1), "pI", "")
    op("G", lambda: g.iota(T.rI[:], [[1, 256]], 0, 0), "rI", "")
    op("G", lambda: g.iota(T.IOTA[:], [[1, W]], 0, 0, allow_small_or_imprecise_dtypes=True), "IOTA", "")
    SH, AND = A.arith_shift_right, A.bitwise_and
    fill("eb", T.eb[:, 2:3], -48.0 * math.log(2.0))
    ts("xI", "pI", T.xI[:], T.pI[:], 15, None, AND)
    ts("hI", "pI", T.hI[:], T.pI[:], 16, None, AND)
    ts("rH", "rI", T.rH[:], T.rI[:, 0:32], 1, None, SH)
    ts("rJ", "rI", T.rJ[:], T.rI[:], 15, None, AND)
    cp("xF", "xI", T.xF[:], T.xI[:])
    cp("hF", "hI", T.hF[:], T.hI[:])
    ts("colA", "xF hF", T.colA[:], T.xF[:], 32.0, T.hF[:], A.mult, A.add)
    ts("L1", "rH xF", T.L1[:], T.rH[:], 16.0, T.xF[:], A.mult, A.add)
    ts("LZ", "rJ colA", T.LZ[:], T.rJ[:, 0:32], T.colA[:], None, A.add)
    cp("of0", "xF", T.of0[:, 0:1], T.xF[:])
    cp("kc2", "slI L1", T.kc2[:], T.slI[:].indirect(T.L1[:, 0:32]))
    vtr("kTa kTb", "kc2", T.kTr[:], T.kc2[:])
    cp("ZT", "kTa kTb LZ", T.ZT[:], T.kTr[:].indirect(T.LZ[:, 0:32]))
    dmas("Y", [(T.Z[j::16, 0:256], T.ZT[j::16, 16 * (5 * j % 16):16 * (5 * j % 16) + 256]) for j in range(16)], "dsh", "Z", "ZT")
    for i in range(2):
        a, b = 1536 * i, 1536 * (i + 1)
        dmas("Y", [(T.recs[:, a:b], T.rec[:, a:b])], "dr%d" % i, "recs%d" % i, "")
    dmas("Y", [(T.Wt[:], T.wealth[:])], "dw", "Wt", "")
    fill("Ed", T.E[:, W:WD], 0.0)
    fill("Kd", T.K[:, W:WD], 0.0)
    ts("rB", "rI", T.rB[:], T.rI[:], 4, None, SH)
    ts("gI", "pI", T.gI[:], T.pI[:], 4, None, SH)
    cp("pF", "pI", T.pF[:], T.pI[:])
    cp("gF", "gI", T.gF[:], T.gI[:])
    ts("ID", "rI pF", T.ID[:], T.rI[:, 0:128], T.pF[:], None, A.is_equal)
    ts("colG", "hF pF", T.colG[:], T.hF[:], -2.0, T.pF[:], A.mult, A.add)
    ts("colG", "colG", T.colG[:], T.colG[:], 16.0, None, A.add)
    ts("SW", "rI colG", T.SW[:], T.rI[:, 0:128], T.colG[:], None, A.is_equal)
    ts("oI", "pI", T.oI[:], T.pI[:], 1, None, AND)
    cp("oF", "oI", T.oF[:], T.oI[:])
    ts("gI", "hI", T.gI[:], T.hI[:], 4, None, SH)
    tt("colF", "oF gI", T.colF[:], T.oF[:], T.gI[:], A.not_equal)
    ts("xI", "xI", T.xI[:], T.xI[:], 1, None, SH)
    ts("colE", "xI hF", T.colE[:], T.xI[:], 32.0, T.hF[:], A.mult, A.add)
    ts("colF", "colF colE", T.colF[:], T.colF[:], 256.0, T.colE[:], A.mult, A.add)
    ts("LP", "rI colF", T.LP[:], T.rI[:, 0:16], T.colF[:], None, A.add)
    LB = math.log(BASE)
    ts("colC", "xF", T.colC[:], T.xF[:], 16.0, None, A.mult)
    ts("colD", "gF", T.colD[:], T.gF[:], 16.0, 15.0, A.mult, A.add)
    tt("colB", "xF hF", T.colB[:], T.xF[:], T.hF[:], A.add)
    ts("lane", "rI xF", T.lane[:], T.rI[:, 0:16], 16.0, T.xF[:], A.mult, A.add)
    fill("eb0", T.eb[:, 0:1], 71.0)
    fill("eb1", T.eb[:, 1:2], 71.0 + math.log(2.53))
    cp("riF", "rI", T.riF[:], T.rI[:])
    act("wcol", "lane eb0", T.wcol[:], T.lane[:], F.Exp, bias=T.eb[:, 0:1], scale=-LB)
    act("THR", "riF eb1", T.THR[:], T.riF[:], F.Exp, bias=T.eb[:, 1:2], scale=-LB)
    ts("Q16", "rI colD", T.Q16[:], T.rI[:, 0:144], T.colD[:], 16.0, A.is_equal, A.mult)
    ts("Q1", "rI colD", T.Q1[:], T.rI[:, 0:144], T.colD[:], None, A.is_equal)
    ts("Q32", "rI colD", T.Q32[:], T.rI[:, 0:144], T.colD[:], 32.0, A.is_equal, A.mult)
    ts("QS", "rI colD", T.QS[:], T.rI[:, 0:144], T.colD[:], 1.0 / 16.0, A.is_equal, A.mult)
    ts("Q1f", "rI colD", T.Q1f[:], T.rI[:, 0:144], T.colD[:], None, A.is_equal)
    ts("BO", "rB gF", T.BO[:], T.rB[:, 0:128], T.gF[:], None, A.is_equal)
    ts("TIE", "rB", T.TIE[:], T.rB[:], -1.0, 15.0, A.mult, A.add)
    ts("DB", "rB xF", T.DB[:], T.rB[:], T.xF[:], None, A.is_equal)
    for i in range(4):
        a, b = 768 * i, 768 * (i + 1)
        cp("K%d" % i, "kinI%d" % i, T.K[:, a:b], T.kinI[:, a:b])
    KK = "K0 K1 K2 K3 Kd"

    def records():
        for i in range(2):
            a, b = 1536 * i, 1536 * (i + 1)
            act("E", "recs%d eb" % i, T.E[:, a:b], T.recs[:, a:b], F.Exp, bias=T.eb[:, 2:3], scale=6.0 * math.log(2.0))

    def later_constants():
        ts("dm", "lane", T.dm[:], T.lane[:], float(W), None, A.add)
        ts("IDf", "rI pF", T.IDf[:], T.rI[:, 0:128], T.pF[:], None, A.is_equal)
        ts("NEG", "rI pF", T.NEG[:], T.rI[:, 0:128], T.pF[:], -1.0, A.is_equal, A.mult)
        for t in range(1, RO):
            ts("um1", "colC", T.um[:, 32 * t + 16:32 * t + 17], T.colC[:], 1.0 / 16.0, 16.0 * t, A.mult, A.add)
        ts("riF", "DB", T.riF[:], T.DB[:], -1e20, 1e20, A.mult, A.add)
        ts("tq", "DB", T.tq[:], T.DB[:], 0.9 * 64.0 ** -3, None, A.mult)
        ts("colE", "xF", T.colE[:], T.xF[:], -1.0, 15.0, A.mult, A.add)
        ts("colF", "oF pF", T.colF[:], T.oF[:], -2.0, T.pF[:], A.mult, A.add)
        tt("DT0", "tq riF", T.DT[:, 0:256], T.tq[:], T.riF[:], A.max)
        ts("OH", "rI colE", T.OH[:], T.rI[:, 0:16], T.colE[:], None, A.is_equal)
        ts("colF", "colF", T.colF[:], T.colF[:], 1.0, None, A.add)
        ts("Dg", "rI xF", T.Dg[:], T.rI[:, 0:16], T.xF[:], 16.0, A.is_equal, A.mult)
        ts("PX", "rI colF", T.PX[:], T.rI[:, 0:128], T.colF[:], None, A.is_equal)
        ts("Ne", "rI xF", T.Ne[:, 0:RO], T.rI[:, 0:RO], T.xF[:], None, A.is_equal)
        ts("Nn", "rI xF", T.Nn[:, 0:RO], T.rI[:, 0:RO], T.xF[:], None, A.not_equal)
        ts("LQ", "rI colB", T.LQ[:], T.rI[:, 0:16], 32.0, T.colB[:], A.mult, A.add)
        ts("L2", "rH colC", T.L2[:], T.rH[:], T.colC[:], None, A.add)
        fill("ON", T.ON[:], 1.0)
        fill("mv", T.mv[:], 0.0)

    def remote(dst, out, in_, rs, r):
        eng = topo.engines(core, dst)[::2]
        m = 0
        for e in eng:
            m |= 1 << e
        rid, pid, _ = topo.addr(dst)
        dep("G", r.split(), [])
        g.remote_dma(out, in_, sem[rs], sem.ls, pid, rid, m)
        cnt["ls"] = cnt.get("ls", 0) + len(eng)
        return len(eng)

    OF = (T.of0, T.of1)

    def draw(t):
        cp("cTu%d" % t, "Z of%d" % (t % 2), T.cTu[:, 16 * t:16 * t + 16], T.Z[:, 0:256].indirect(OF[t % 2][:, 0:1]))

    ident = T.ID[:]
    Ew, Kw, Ww, Iw = T.E[:, 0:W], T.K[:, 0:W], T.Wt[:], T.IOTA[:]

    def gather_e(eng, dst, dk, lst, lk, a, n):
        out, in_ = dst[:, 16 * a:16 * (a + n)], Ew.indirect(lst[:, a:a + n])
        if eng == "S":
            act(dk, "E " + lk, out, in_)
        else:
            cp(dk, "E " + lk, out, in_)

    def sum_e(ps, pk, dst, dk, a, n, st, sp):
        for m in range(16):
            mm(pk, dk + " ID", ps[:, a:a + n], ident, dst[:, 16 * a + m:16 * (a + n):16], st and m == 0, sp and m == 15)

    draw(0)
    for t in range(RO):
        asked = T.cores[(rank + 1 + t % 3) % 4]
        asker = T.cores[(rank - 1 - t % 3) % 4]
        cu = T.cTu[:, 16 * t:16 * t + 16]
        cuk = "cTu%d" % t
        cfk, cf = ("cTf", T.cTf) if t % 2 == 0 else ("cTg", T.cTg)
        last = t == RO - 1
        u = 32 * (t + 1)
        dtk, dt_ = "DT%d" % (t % 2), T.DT[:, 256 * (t % 2):256 * (t % 2) + 256]
        ne = remote(asked, T.ql[:, 16 * t:16 * t + 16], cu, "qa%d" % t, cuk)
        lastw["ql%d" % t] = ("qa%d" % t, ne)
        lastw["rl%d" % t] = ("ra%d" % t, ne)
        act(cfk, "Z of%d" % (t % 2), cf[:], T.Z[:, 0:256].indirect(OF[t % 2][:, 0:1]))
        act("kcf", KK + " " + cuk, T.kcf[:], Kw.indirect(cu))

        def own_wealth():
            act("wc", "Wt " + cuk, T.wc[:, 0:256], Ww.indirect(cu))
            act("wcb", "Wt " + cuk, T.wc[:, 256:512], Ww.indirect(cu))
        if t == 0:
            records()
        else:
            own_wealth()
            tt("E Ed", "Ec DBt SL", T.E[:].indirect(T.SL[:]), T.Ec[:], T.DBt[:, 0:256], A.add)
        cp("kcu", "kcf", T.kcu[:], T.kcf[:])
        act("Ec", "E " + cuk, T.Ec[:], Ew.indirect(cu))
        vtr("kTa", "kcf", T.kTr[:, 0:256], T.kcf[:])
        mm("pX", "kTa SW", T.pX[:, 0:256], T.SW[:], T.kTr[:, 0:256], True, True)
        act("kTb", "pX", T.kTr[:, 256:512], T.pX[:, 0:256])
        cp("cbu", "IOTA " + cuk, T.cbu[:], Iw.indirect(cu))
        gather_e("S", T.GE, "GE0", T.kcu, "kcu", 0, 64)
        if t == 0:
            own_wealth()
            later_constants()
        mm("pES", "Ec ID", T.pES[:, 0:256], ident, T.Ec[:], True, False)
        sum_e(T.pES, "pES", T.GE, "GE0", 0, 64, False, False)

        def equal(b):
            o, n = XB[b], 256 - 16 * b
            ts("EQT%d" % b, "cbu wcol " + cfk, T.EQT[:, o:o + n], T.cbu[:, 16 * b:256], cf[:, b:b + 1], T.wcol[:, b:b + 1], A.is_equal, A.mult)

        def equal_sum(b):
            o, n = XB[b], 256 - 16 * b
            mm("pEQ", "EQT%d BO" % b, T.pEQ[:, 16 * b:256], T.BO[:], T.EQT[:, o:o + n], b == 0, b == 15)

        def wealth(m):
            tt("X%d" % m, "Wt kTu wc wcb", T.X[:, 512 * m:512 * m + 512], Ww.indirect(T.kTu[:, 32 * m:32 * m + 32]), T.wc[:], A.max)

        def score(h):
            mm("pS1", "TIE ID", T.pS1[:, 128 * h:128 * h + 128], ident, T.TIE[:, 128 * h:128 * h + 128], True, False)
            xs = " ".join("X%d" % m for m in range(4 * h, 4 * h + 4))
            for j in range(16):
                mm("pS1", xs + " Q16", T.pS1[:, 128 * h:128 * h + 128], T.Q16[:, 15 - j:143 - j], T.X[:, 2048 * h + j:2048 * h + 2048:16], False, j == 15)
        for b in range(EQ1):
            equal(b)
        cp("kTu", "kTa kTb LP", T.kTu[:], T.kTr[:].indirect(T.LP[:]))
        cp("fku", KK + " ql%d" % t, T.fku[:], Kw.indirect(T.ql[:, 16 * t:16 * t + 16]))
        for m in range(WV):
            wealth(m)
        gather_e("V", T.FE, "FE3", T.fku, "fku", 192, 64)
        for m in range(WV, 8):
            wealth(m)
        for b in range(EQ1):
            equal_sum(b)
        for k in range(3):
            gather_e("S", T.FE, "FE%d" % k, T.fku, "fku", 64 * k, 64)
        for k in range(4):
            if k == KS:
                score(0)
            p = (0, 1, 3, 2)[k]
            sum_e(T.pFS, "pFS", T.FE, "FE%d" % p, 64 * p, 64, True, True)
        gather_e("S", T.GE, "GE1", T.kcu, "kcu", 64, 32)
        fs = T.fs[:, 256 * t:256 * t + 256]
        act("fs%d" % t, "pFS", fs, T.pFS[:, 0:256])
        remote(asker, T.rl[:, 256 * t:256 * t + 256], fs, "ra%d" % t, "fs%d" % t)
        score(1)
        gather_e("S", T.GE, "GE1b", T.kcu, "kcu", 96, 32)
        gather_e("S", T.GE, "GE2", T.kcu, "kcu", 128, 64)
        act("S1s", "pS1", T.S1s[:], T.pS1[:, 128:256])
        if NV < 64:
            gather_e("S", T.GE, "GE3", T.kcu, "kcu", 192, 64 - NV)
        for b in range(EQ1, 16):
            equal(b)
            equal_sum(b)
        sum_e(T.pES, "pES", T.GE, "GE1 GE1b", 64, 64, False, False)
        if not last:
            mm("pX", "PX " + cfk, T.pX[:, 0:16], T.PX[:], cf[:], True, True)
        mm("pX", "IDf " + cfk, T.pX[:, 16:32], T.IDf[:], cf[:], True, False)
        mm("pX", "NEG dm", T.pX[:, 16:32], T.NEG[:], T.dm[:], False, True)
        if NV:
            gather_e("V", T.GE, "GE4", T.kcu, "kcu", 256 - NV, NV)
        tt("cb", "pEQ THR", T.cb[:], T.pEQ[:, 0:256], T.THR[:], A.is_lt)
        if not last:
            cp("cTs", "pX", T.cTs[:], T.pX[:, 0:16])
        sum_e(T.pES, "pES", T.GE, "GE2", 128, 64, False, False)
        tt("t1", "pS1 S1s", T.t1[:], T.pS1[:, 0:128], T.S1s[:], A.max)
        sum_e(T.pES, "pES", T.GE, "GE3 GE4", 192, 64, False, False)
        mm("pES", "rl%d ID" % t, T.pES[:, 0:256], ident, T.rl[:, 256 * t:256 * t + 256], False, True)
        for j in range(16):
            mm("pX", "cb QS", T.pX[:, 32:48], T.QS[:, 15 - j:143 - j], T.cb[:, j::16], j == 0, j == 15)
        act("cs", "pX", T.cs[:], T.pX[:, 32:48])
        tt("t2", "t1", T.t2[:], T.t1[:, 0:64], T.t1[:, 64:128], A.max)
        mm("pB", "IDf " + cfk, T.pB[:, 32:47], T.IDf[:], cf[:, 0:15], True, False)
        mm("pB", "NEG " + cfk, T.pB[:, 32:47], T.NEG[:], cf[:, 1:16], False, True)
        tt("t3", "t2", T.t1[:, 0:32], T.t2[:, 0:32], T.t2[:, 32:64], A.max)
        if not last:
            act("kcm", "kcf Nn", T.kcm[:], T.kcf[:], F.Copy, scale=T.Nn[:, t:t + 1])
            act("cXm", "IOTA Ne cTs", T.cXm[:], Iw.indirect(T.cTs[:]), F.Copy, scale=T.Ne[:, t:t + 1])
        act("DBt", "DB", T.DBt[:, 0:256], T.DB[:], F.Copy, scale=64.0 ** t)
        if not last:
            o = 256 * ((t + 1) % 2)
            act("DT%d" % ((t + 1) % 2), dtk, T.DT[:, o:o + 256], dt_, F.Copy, scale=64.0)
        ts("X1", "pES", T.X1[:], T.pES[:, 0:256], 0.9 * 64.0 ** (t - 2), 0.5, A.is_ge, A.subtract)
        for j in range(16):
            mm("pZ", "X1 Q1", T.pZ[:, 0:16], T.Q1[:, 15 - j:143 - j], T.X1[:, j::16], j == 0, False)
        tt("X2", "pES " + dtk, T.X2[:], T.pES[:, 0:256], dt_, A.is_ge)
        for j in range(16):
            mm("pZ", "X2 Q32", T.pZ[:, 0:16], T.Q32[:, 15 - j:143 - j], T.X2[:, j::16], False, j == 15)
        tt("bI", "t3", T.bI[:], T.t1[:, 0:16], T.t1[:, 16:32], A.max)
        ts("bI2", "bI", T.bI2[:], T.bI[:], 15, None, AND)
        cp("mu", "bI2", T.mu[:], T.bI2[:])
        tt("Pm", "OH mu kcf", T.Pm[:], T.OH[:].indirect(T.mu[:]), T.kcf[:], A.mult)
        tt("zc", "pZ cs", T.zc[:], T.pZ[:, 0:16], T.cs[:], A.mult)
        ts("a1", "zc", T.a1[:], T.zc[:], 0.0, None, A.is_lt)
        ts("z4", "zc", T.z4[:], T.zc[:], -4.0, None, A.add)
        if not last:
            mm("pU", "a1 ON", T.pU[:, 0:16], T.ON[:], T.a1[:], True, True)
        mm("pB", "NEG " + cfk, T.pB[:, 0:16], T.NEG[:], cf[:], True, False)
        for j in range(16):
            mm("pB", "Pm Q1f", T.pB[:, 0:16], T.Q1f[:, 15 - j:143 - j], T.Pm[:, j::16], False, j == 15)
        tt("m1", "pX a1", T.m1[:], T.pX[:, 16:32], T.a1[:], A.mult)
        ts("zy", "z4", T.zy[:], T.z4[:], 31, None, AND)
        ts("od", "z4", T.od[:], T.z4[:], 1, None, AND)
        tt("m2", "m1 dm", T.m2[:], T.m1[:], T.dm[:], A.add)
        ts("b3", "zy", T.b3[:], T.zy[:], 5.0, None, A.is_lt)
        if not last:
            tt("um0", "pU Dg", T.um[:, u:u + 16], T.pU[:, 0:16], T.Dg[:], A.mult)
        tt("tn", "a1 b3", T.tn[:], T.a1[:], T.b3[:], A.add)
        cp("SL", "m2", T.SL[:], T.m2[:])
        if not last:
            op("V", lambda: g.vector.tensor_reduce(T.um[:, u + 17:u + 18], T.um[:, u:u + 17], AxisListType.X, A.add), "um2", "um0 um1")
        tt("mv0", "od tn", T.mv0[:], T.od[:], T.tn[:], A.is_gt)
        if not last:
            ts("uk", "um2", T.uk[:], T.um[:, u + 17:u + 18], 1.0 / 256.0, -127.5 / 256.0, A.mult, A.add)
        tt("mv", "mv0 tn", T.mv[:, 0:15], T.mv0[:, 0:15], T.tn[:, 1:16], A.mult)
        if not last:
            ts("of%d" % ((t + 1) % 2), "uk um2", OF[(t + 1) % 2][:, 0:1], T.uk[:], -256.0, T.um[:, u + 17:u + 18], A.mult, A.add)
        tt("tm", "mv tn", T.tm[:], T.tn[:], T.mv[:], A.add)
        if not last:
            tt(KK, "kcm cXm SL", T.K[:].indirect(T.SL[:]), T.kcm[:], T.cXm[:], A.add)
        else:
            tt("E Ed", "Ec DBt SL", T.E[:].indirect(T.SL[:]), T.Ec[:], T.DBt[:, 0:256], A.add)
        tt("tm", "tm mv", T.tm[:, 1:16], T.tm[:, 1:16], T.mv[:, 0:15], A.subtract)
        tt("v1", "mv pB", T.v1[:, 0:15], T.mv[:, 0:15], T.pB[:, 32:47], A.mult)
        tt("u1", "tm pB", T.u1[:], T.tm[:], T.pB[:, 0:16], A.mult)
        tt("nT", "u1 " + cfk, T.nT[:], T.u1[:], cf[:], A.add)
        tt("nT", "nT v1", T.nT[:, 1:16], T.nT[:, 1:16], T.v1[:, 0:15], A.add)
        cp("Z", "nT of%d" % (t % 2), T.Z[:, 0:256].indirect(OF[t % 2][:, 0:1]), T.nT[:])
        if not last:
            draw(t + 1)

    cp("Z2", "Z", T.Z[:, 256:512], T.Z[:, 0:256])
    dmas("Y", [(T.ZT[j::16, 0:256], T.Z[j::16, 16 * (-5 * j % 16):16 * (-5 * j % 16) + 256]) for j in range(16)], "dun", "ZT", "Z Z2")
    for i in range(4):
        a, b = 768 * i, 768 * (i + 1)
        act("LN%d IOTA" % i, "E", T.IOTA[:, a:b], T.E[:, a:b], F.Ln)
        if i == 3:
            act("YR3", "LN3", T.Wt[:, a:b], T.IOTA[:, a:b], F.Identity, bias=136.0, scale=1.0 / (6.0 * math.log(2.0)))
        else:
            ts("YR%d" % i + ("" if i else " Wt"), "LN%d" % i, T.Wt[:, a:b], T.IOTA[:, a:b], 1.0 / (6.0 * math.log(2.0)), 136.0, A.mult, A.add)
        ts("YQ%d" % i, "YR%d" % i, T.recs[:, a:b], T.Wt[:, a:b], -128.0, None, A.add)
        dmas("Y", [(T.yr[:, a:b], T.recs[:, a:b])], "dy%d" % i, "", "YQ%d" % i)
    cp("kc2", "ZT L2", T.kc2[:], T.ZT[:, 0:256].indirect(T.L2[:, 0:32]))
    vtr("kTa kTb", "kc2", T.kTr[:], T.kc2[:])
    cp("Pm", "kTa kTb LQ", T.Pm[:], T.kTr[:].indirect(T.LQ[:]))
    dmas("Y", [(T.ys[:], T.Pm[:])], "dys", "", "Pm")
    for s in cnt:
        if clock["G"].get(s, 0) < cnt[s]:
            g.wait_ge(sem[s], cnt[s])
